import numpy as np, ml_dtypes
CORES = [16,18,20,22]
N = 4
BF = ml_dtypes.bfloat16
def gentries(a):
    return np.ascontiguousarray(a.reshape(8, 16, -1).transpose(0, 2, 1)).reshape(8, -1)
def gtable(e):
    e = np.asarray(e); return np.ascontiguousarray(e.reshape(8, -1, 16).transpose(0, 2, 1)).reshape(128, -1).astype(np.int32)
W, D, L, B, K, RO, Q = 4096, 16, 256, 16, 4096, 5, 2
def join(p, c):
    return (((p * c) >> 5) + p + 37 * c) & (W - 1)
def parts(rng):
    x = rng.integers(0, 256, (N, 8, 16, W)); p = rng.integers(0, W, (N, 8, D, L)); c = rng.integers(0, W, (N, 8, D, L))
    c = np.where(rng.random(c.shape) < 0.0625, p, c); s = rng.integers(1, 65, (N, 8, 1, L))
    n = (rng.integers(0, 256, (N, 8, 16, L)) * s * s) >> 12
    return x, p, c, n, rng.integers(0, 64, (N, 8, 16)), rng.integers(1100, 1800, (N, 8))
def pack(x, p, c, n, w, t):
    return {"lit": np.ascontiguousarray(x.reshape(N, 128, W)).astype(np.float32).astype(BF), "pn": np.stack([gtable(a) for a in p.reshape(N, 8, K)]), "cn": np.stack([gtable(a) for a in c.reshape(N, 8, K)]),
            "neg": np.ascontiguousarray(n.reshape(N, 128, L)).astype(np.float32).astype(BF), "wt": w.reshape(N, 128, 1).astype(np.int32), "th": t.reshape(N, 8, 1).astype(np.int32)}
def pat(rng, m):
    return ((np.arange(16)[:, None] * (2 * rng.integers(0, 8, m.shape) + 1) + rng.integers(0, 16, m.shape)) & 15) < m
def setup_inputs(rng):
    return pack(*parts(rng))
def setup_inputs_spread(rng):
    x, p, c, n, w, t = parts(rng)
    x = rng.integers(0, 256, x.shape) >> rng.integers(0, 8, (N, 8, 1, W)); n = rng.integers(0, 256, n.shape) >> rng.integers(0, 8, (N, 8, 1, L))
    p = np.minimum((W * rng.random(p.shape) ** 3).astype(np.int64), W - 1); c = np.minimum((W * rng.random(c.shape) ** 2).astype(np.int64), W - 1)
    w = w >> rng.integers(0, 6, w.shape); t = np.minimum(np.exp2(12 * rng.random((N, 8))).astype(np.int64), 4080)
    return pack(x, p, c, n, w, t)
def setup_inputs_ends(rng):
    cho = np.array([0, 1, 7, 8, 9, 10, 15, 16])
    x = 255 * pat(rng, rng.choice(cho, (N, 8, 1, W))); n = 255 * pat(rng, rng.choice(cho, (N, 8, 1, L)))
    p = (W - 1) * rng.integers(0, 2, (N, 8, D, L)); c = (W - 1) * rng.integers(0, 2, (N, 8, D, L))
    w = 63 * rng.integers(0, 2, (N, 8, 16)); w[:, 0] = 0; w[:, 7] = 63
    t = 4080 * ((np.arange(8)[None, :] + np.arange(N)[:, None] + N + 1) & 1)
    x[:, 1::2, :, 0] = 0; x[:, 1::2, :, W - 1] = 255; x[:, 2, :, 0] = 255; x[:, 2, :, W - 1] = 0
    x[:, 7, :, int(join(W - 1, W - 1))] = 255
    for i in (0, 1, L - 1): p[:, 7, :, i] = W - 1; c[:, 7, :, i] = W - 1; n[:, 7, :, i] = 255
    for i in (2, L - 2): p[:, 7, :, i] = W - 1; c[:, 7, :, i] = 0; n[:, 7, :, i] = 255
    return pack(x, p, c, n, w, t)
def setup_inputs_corners(rng):
    x, p, c, n, w, t = parts(rng)
    a = np.arange(W // 2); a = a[join(a, a) >= W // 2]; m = len(a) // 6; F = np.ascontiguousarray(a[:6 * m].reshape(m, 6).T)
    o = np.argsort(rng.random((N, 8, 16)), axis=-1)[..., None]; sh = (N, 8, 16, m); u = rng.random(sh)
    low = [u < 0, (o < 7) & (u < 2), (o < 7) & (u < 0.3), (o == rng.integers(7, 16, (N, 8, 1, m))), (o < 8) | (u < 0.3), u < 0.25]
    for f in range(6):
        hi = 100 + rng.integers(0, 156, sh) * rng.integers(0, 2, sh); lo = 99 - rng.integers(0, 100, sh) * rng.integers(0, 2, sh)
        x[..., F[f]] = np.where(low[f], lo, hi)
    x[..., W // 2:] = rng.integers(100, 256, (N, 8, 16, W - W // 2))
    ty = rng.integers(0, 6, (N, 8, 1, L)); j = np.arange(D)[None, None, :, None]; pl = rng.integers(0, D - 1, (N, 8, 1, L))
    fam = 2 * rng.integers(0, 2, (N, 8, D, L))
    fam = np.where((ty == 0) & (j == 0), 4, fam); fam = np.where(ty == 1, 0, fam)
    fam = np.where(((ty == 2) | (ty == 3)) & (j == pl), 1, fam); fam = np.where((ty == 2) & (j == D - 1), 3, fam)
    fam = np.where(ty == 4, 5, fam); fam = np.where(ty == 5, rng.integers(0, 4, fam.shape), fam)
    free = rng.random((N, 8, 1, L)) < 0.125
    p = F[fam, rng.integers(0, m, fam.shape)]; c = np.where(free, c, p); n = np.where(free, n, 100)
    w[:, 0] = 0; w[:, 1] = 63; w[:, 2::2] = 63 * rng.integers(0, 2, (N, 3, 16))
    t = rng.choice(np.array([0, 63, 1365, 4080]), (N, 8)); t[:, 3] = 0; t[:, 5] = 4080
    return pack(x, p, c, n, w, t)
def setup_inputs_ties(rng):
    x, p, c, n, w, t = parts(rng); h = W // 2
    t = rng.integers(200, 1600, (N, 8)); t[:, 3] = rng.choice(np.array([2048, 2051, 3000, 3001, 3003, 4016, 4063, 4064]), N); t[:, 5] = rng.integers(2048, 4079, N); t[:, 7] = 4079
    tot = t[..., None, None] + rng.integers(-1, 2, (N, 8, 1, h))
    d = (tot >> 4) + (np.arange(16)[:, None] < (tot & 15))
    u = np.minimum(rng.integers(0, 12, (N, 8, 8, h)), np.minimum(255 - d[:, :, 0::2], d[:, :, 1::2]))
    d[:, :, 0::2] += u; d[:, :, 1::2] -= u
    lo = (np.minimum(144, 256 - d) * rng.random(d.shape)).astype(np.int64); hi = lo + d; sg = rng.random(lo.shape) < 0.5
    x[..., 0::2] = np.where(sg, hi, lo); x[..., 1::2] = np.where(sg, lo, hi)
    free = rng.random((N, 8, 1, L)) < 0.125; a = 2 * rng.integers(0, h, (N, 8, D, L)); b = rng.integers(0, 2, (N, 8, D, L))
    p = np.where(free, p, a + b); c = np.where(free, c, a + 1 - b)
    v = np.full((N, 8, 16, L), 255)
    for k in range(2):
        e = [np.take_along_axis(x, i[:, :, None, :], 3) for i in (p[:, :, k], c[:, :, k], join(p[:, :, k], c[:, :, k]))]
        v = np.minimum(v, np.minimum(np.maximum(e[0], e[1]), e[2]))
    n = np.where(free, n, np.minimum(v + (rng.random(v.shape) < 0.3), 255))
    return pack(x, p, c, n, w, t)
def setup_inputs_crowd(rng):
    x, p, c, n, w, t = parts(rng); x = np.minimum(x, 254); top = np.array([7, 7, 7, 7, 3, 3, 3, 3])
    calm = np.where(pat(rng, np.full((N, 8, 1, L), 9)), 0, rng.integers(1, 256, n.shape))
    for q in range(N):
        for g in range(8):
            i = int(rng.integers(0, L)); col = rng.integers(0, W, 4)
            if g % 4 == 0: p[q, g] = col[0]; c[q, g] = col[1]
            if g % 4 == 1:
                own = p[q, g, :, i].copy(); p[q, g] = col[0]; p[q, g, :, i] = own
            if g % 4 == 2: p[q, g] = col[rng.integers(0, 4, (D, L))]; c[q, g] = col[rng.integers(0, 4, (D, L))]
        k = (3 - q) % 4; n[q] = calm[q] if k < 2 else 255
        g, i = int(rng.integers(0, 8)), int(rng.integers(0, L))
        if k == 1:
            x[q] = x[q] & top[:, None, None]; n[q] = np.minimum(n[q], top[:, None, None]); t[q] = np.maximum(16 * top - 63, 0)
            n[q, g, :, i] = top[g] + 1
        if k == 2: x[q] = 127 + (x[q] >> 1)
        if k == 3: n[q, g, :, i] = calm[q, g, :, i]
    c[:, :, 0] = p[:, :, 0]
    return pack(x, p, c, n, w, t)
def check_inputs(d):
    bad = []
    for k, lo, hi in (("lit", 0, 255), ("pn", 0, W - 1), ("cn", 0, W - 1), ("neg", 0, 255), ("wt", 0, 63), ("th", 0, 4080)):
        v = np.asarray(d[k]).astype(np.float64)
        if not np.all((v >= lo) & (v <= hi)): bad.append("range of " + k)
        elif np.any(v != np.floor(v)): bad.append("whole numbers in " + k)
    return bad
def pick(v, ix):
    return np.stack([v[g][:, ix[g]] for g in range(8)])
def reference(lit, pn, cn, neg, wt, th):
    X = lit.astype(np.float32).astype(np.int16).reshape(N, 8, 16, W); n = neg.astype(np.float32).astype(np.int16).reshape(N, 8, 16, L)
    P = np.stack([gentries(a) for a in pn]).astype(np.int64); C = np.stack([gentries(a) for a in cn]).astype(np.int64)
    w = wt.astype(np.int64).reshape(N, 8, 16, 1); lim = th.astype(np.int64).reshape(N, 8, 1); A = [0] * N
    j = np.arange(D)[None, :, None]
    for t in range(RO):
        newp, names, mins = [], [], []
        for r in range(N):
            h = join(P[r], C[r]); x, y, z = pick(X[r], P[r]), pick(X[r], C[r]), pick(X[r], h)
            ok = np.add.reduce(np.abs(x - y), axis=1, dtype=np.int64) <= lim[r] + (A[r] & 63)
            l = np.where(ok[:, None, :], np.minimum(np.maximum(x, y), z), np.int16(255)).reshape(8, 16, D, L)
            nm = np.where(ok, h, P[r]).reshape(8, D, L); fell = np.zeros((8, D, L), bool); esc = np.zeros((8, L), bool)
            for s in range(Q):
                M = np.minimum.accumulate(l, axis=2)
                blk = np.add.reduce(M >= n[r][:, :, None, :], axis=1, dtype=np.int64) < 9
                has = np.any(blk, axis=1)[:, None, :]; ks = np.argmax(blk, axis=1)[:, None, :]
                if s == 0: esc = ~has[:, 0]
                turn = has & (j <= ks); cut = has & (j > ks)
                nm = np.where(turn, np.concatenate([np.take_along_axis(nm, ks, 1), nm[:, :-1]], axis=1), nm)
                l = np.where(turn[:, None], np.concatenate([np.take_along_axis(l, ks[:, None], 2), l[:, :, :-1]], axis=2), l)
                l = np.where(cut[:, None], np.int16(255), l); fell = fell | cut
            m = np.minimum.reduce(l, axis=2)
            place = B * np.arange(L)[None, :] + (np.add.reduce(w[r] * m, axis=1) & (B - 1))
            val = (m + n[r]) >> 1
            for g in range(8): X[r, g][:, place[g]] = val[g]
            A[r] = int(np.count_nonzero(esc))
            newp.append(np.where(fell, C[r].reshape(8, D, L), nm).reshape(8, K))
            names.append(nm.reshape(8, K)); mins.append(np.where(esc[:, None, :], n[r], m))
        d = 1 + t % 3
        P = np.stack(newp); C = np.stack([names[(r - d) % N] for r in range(N)]); n = np.stack([mins[(r - d) % N] for r in range(N)])
    yx = X.reshape(N, 128, W).astype(np.float32).astype(BF)
    return {"yp": np.stack([gtable(a) for a in P]).astype(np.float32), "yc": np.stack([gtable(a) for a in C]).astype(np.float32), "yn": n.reshape(N, 128, L).astype(np.float32).astype(BF), "yx": yx}

@@ -1,0 +1,658 @@
+import numpy as np
+from concourse.mybir import AluOpType as A, ActivationFunctionType as F
+
+RO, NL = 5, 256
+CFG = dict(FC=[64, 64, 64, 64], BC=[128, 128], HC=[128, 128], XV=(1,), YV=(), MXP=(), ZA=(), PS=(0, 1, 2), DA=False,
+           GS={0: [16, 48]}, LS={3: [32, 32]}, CA=(), VA=(0,), SA=(0, 1))
+PRIO = {}
+PR = "jzj8jfk8hgiqlkiymdkpkgizjvn1nvl8khlpk2k0jxgyhdjdl3ksiqihhxhfjnkajnkdjlktkfkojujvlnksl5kxk0jll6l6kckpkknah8hxiaiynekdh5kdjglxmajfjyjaiqkohlh2gbhhjhmhnniulalfkulohij5jmkei2jfhhhohdhhhahhh5ighjiniflqmumqmpishxi1jfkulxlnlyl1kqnio2hrisi7i1h9hvjxichqhyhxhyi0hdkzkxixhsj2jak5kgk3m5kthvl8icjuh2hrhlhvh1icjwk4jojfh5h4hkh8hoiahzhyi1h5i9hvjzi5iyiihoigighzi3ijjajaich4hjifjhj9hzhxjhirjojbhiijifhvhtiziyjbkekekcg9gqk9iokrj9i1mzobsco3mdl8l2lvhckrj3j3l7jkigguiuitjpj7haiehaimhlitghk1kll1kdhtjej2jii9ithdifhhhojijyh7h4i2hcidjjiljli8i6jdhhhkh3ibibgaiihpiwfxi9hpefengcglg6"
+BF, F32, I32, U16 = "bfloat16", "float32", "int32", "uint16"
+
+
+def sb(n, d):
+    return ("sbuf", [128, n], d)
+
+
+SCRATCH = {
+    "X": sb(4112, BF), "xb": sb(4096, BF), "yb": sb(4096, BF), "mx": sb(4096, BF), "lp": sb(4096, BF), "la": sb(4096, BF),
+    "Mw": sb(4096 + 64, BF), "zb": sb(4096, BF), "Td": sb(128, F32), "on": sb(128, F32), "Bb": sb(4112, BF), "B2": sb(4096, BF), "Rs": sb(2048, BF),
+    "pci": sb(512, I32), "t1": sb(1024, F32), "t2": sb(1024, F32), "yo": sb(512, F32),
+    "CF": sb(256 * (RO + 1), F32), "NN": sb(256 * (RO + 1), BF), "SC": sb(256 * RO, F32), "SM": sb(256 * RO, BF),
+    "pf": sb(256, F32), "pp": sb(256, F32), "pu": sb(256, U16), "cu": sb(256, U16), "hu": sb(256, U16),
+    "tq": sb(256, F32), "vi": sb(256, I32), "hi": sb(256, I32), "a1": sb(256, F32), "Nf": sb(256, F32),
+    "Ds": sb(256, F32), "ta": sb(256, F32), "tb": sb(256, F32), "nb": sb(256, BF), "kp": sb(256, BF),
+    "lk": sb(256, BF), "Mm": sb(256, BF), "nh": sb(256, BF), "vl": sb(256, I32),
+    "i1": sb(16, U16), "i2": sb(16, U16), "i3": sb(16, U16), "qq": sb(16, I32), "ff": sb(16, F32),
+    "acc": sb(8, F32), "ai": sb(4, I32), "bz": sb(4, F32),
+    "wi": sb(1, I32), "ti": sb(1, I32), "tf": sb(4, F32), "pi": sb(4, I32), "col": sb(24, F32), "nz": sb(2, BF),
+    "Mi": sb(144, F32), "Mg": sb(128, F32), "Ja": sb(32, F32),
+    "oA": sb(32, U16), "oB": sb(16, U16), "oC": sb(32, U16), "oD": sb(16, U16), "b16": sb(16, BF), "bi": sb(16, F32),
+    "Ib": sb(128, BF), "In": sb(128, BF), "Ih": sb(128, BF), "Am": sb(128, BF), "En": sb(128, BF), "Ep": sb(128, BF), "Em": sb(128, BF),
+    "SZ": sb(144, BF), "SH": sb(144, BF), "S8": sb(144, BF), "SW": sb(144, BF), "S1": sb(144, BF), "S2": sb(144, BF),
+    "K1": sb(128, BF), "K2": sb(128, BF), "KW": sb(128, BF), "Cz": sb(128, BF), "Cb": sb(128, BF), "R0": sb(128, F32), "Ml": sb(128, F32),
+    "pk": sb(256, F32), "vf": sb(256, F32), "vb": sb(256, BF),
+    "If": sb(128, F32), "Dm": sb(128, F32), "Dt": sb(128, F32), "Wm": sb(128, F32), "DW": sb(128, F32), "Sa": sb(128, F32), "G8": sb(128, F32),
+}
+for _b in range(8):
+    SCRATCH["ps%d" % _b] = ("psum", [128, 512], F32)
+SEMAPHORES = ["cv", "ca", "cp", "cg", "loc"] + ["d%d" % i for i in range(24)] + ["r%d" % i for i in range(8 * RO)]
+
+COST = dict(G=1.56, S=3.8, tt2=1.0, cyc=0.83 * 1.2, pe=0.42 * 1.2, fv=60.0, fa=70.0, fp=10.0, hop=90.0, rem=2200.0)
+
+
+def V(name, c0=0, c1=None, st=1, p0=0, p1=128, off=None):
+    if c1 is None:
+        c1 = SCRATCH[name][1][1]
+    return dict(name=name, c0=c0, c1=c1, st=st, p0=p0, p1=p1, off=off)
+
+
+def IND(win, off):
+    w = dict(win)
+    w["off"] = off
+    return w
+
+
+def width(v):
+    if v["off"] is not None:
+        return 16 * width(v["off"])
+    return (v["c1"] - v["c0"] + v["st"] - 1) // v["st"]
+
+
+def ap(T, v):
+    if not isinstance(v, dict):
+        return v
+    t = T[v["name"]]
+    r = t[v["p0"]:v["p1"], v["c0"]:v["c1"]] if v["st"] == 1 else t[v["p0"]:v["p1"], v["c0"]:v["c1"]:v["st"]]
+    if v["off"] is not None:
+        return r.indirect(ap(T, v["off"]))
+    return r
+
+
+def isps(v):
+    return v["name"].startswith("ps")
+
+
+def two(v):
+    return SCRATCH[v["name"]][2] in (BF, U16)
+
+
+def spans(vs):
+    out = []
+    for v in vs:
+        if isinstance(v, dict):
+            out.append((v["name"], v["c0"], v["c1"]))
+            if v["off"] is not None:
+                out.append((v["off"]["name"], v["off"]["c0"], v["off"]["c1"]))
+    return out
+
+
+def build(cfg):
+    ops = []
+    FC, BC, HC = cfg["FC"], cfg["BC"], cfg["HC"]
+    now, grp = ["s", set()], ["s"]
+
+    def add(eng, kind, args, outs, ins, n, **kw):
+        w = [(v["name"], v["c0"], v["c1"]) for v in outs]
+        r = spans(ins) + [(v["off"]["name"], v["off"]["c0"], v["off"]["c1"]) for v in outs if v["off"] is not None]
+        nm, c = (w or r)[0][:2]
+        key = "%s%s%d" % (now[0], nm, c % 256 if nm in ("CF", "NN", "SC", "SM") else c)
+        while key in now[1]:
+            key += "+"
+        now[1].add(key)
+        ops.append(dict(eng=eng, kind=kind, args=args, w=w, r=r, n=n, key=key, grp=grp[0], **kw))
+
+    def vcost(out, ins, tt=False):
+        n = width(out)
+        if out["off"] is not None:
+            return ("S", n)
+        if ins and ins[0]["off"] is not None:
+            return ("G", n)
+        allb = two(out) and all(two(v) for v in ins)
+        if tt and not any(isps(v) for v in ins):
+            return ("tt2", n) if allb else ("c", 2 * n)
+        return ("c", n / 2 if allb else n)
+
+    def cp(out, a):
+        add("v", "cp", (out, a), [out], [a], vcost(out, [a]))
+
+    def tt(out, a, b, op):
+        add("v", "tt", (out, a, b, op), [out], [a, b], vcost(out, [a, b], True))
+
+    def ts(out, a, s1, op0, s2=None, op1=None):
+        add("v", "ts", (out, a, s1, s2, op0, op1), [out], [a, s1, s2], vcost(out, [a]))
+
+    def scan(out, d0, d1):
+        add("v", "scan", (out, d0, d1), [out], [d0, d1], vcost(out, [d0, d1]))
+
+    def ms(out, c):
+        add("v", "ms", (out, c), [out], [], vcost(out, []))
+
+    def tr(out, a):
+        add("v", "tr", (out, a), [out], [a], vcost(out, [a]))
+
+    def act(out, a, f, bias=0.0, scale=1.0, acc=None, extra=0.0):
+        add("a", "act", (out, a, f, bias, scale, acc), [out] + ([acc] if acc else []), [a, bias, scale],
+            ("G" if a["off"] is not None else "c", width(out)), extra=extra)
+
+    def mm(lst, start=True, stop=True, tok=None):
+        n = sum(max(64, width(m[0])) * (1 if two(m[2]) else 4) for m in lst)
+        add("p", "mm", lst, [m[0] for m in lst], [m[1] for m in lst] + [m[2] for m in lst], ("pe", n), cnt=len(lst), start=start, stop=stop)
+        if tok is not None:
+            ops[-1]["w"].append((tok, 0, 1))
+
+    def iota(out, pat, cm):
+        add("g", "iota", (out, pat, cm), [out], [], ("c", 160 + 2 * width(out)))
+
+    nd = [0, 0]
+
+    def load(q, out, name, us):
+        add(q, "load", (out, name), [out], [], ("dma", us), sem="d%d" % nd[0])
+        nd[0] += 1
+
+    def store(q, name, c0, c1, a, us):
+        add(q, "store", (name, c0, c1, a), [], [a], ("dma", us), sem="d%d" % nd[0], last=True)
+        nd[0] += 1
+
+    def send(dst, src, t):
+        add("g", "send", (dst, src, t), [dst], [src], ("rem", 0), sem="r%d" % nd[1])
+        nd[1] += 1
+
+    def col(j):
+        return V("col", j, j + 1)
+
+    SIG, ZC, QR, UP, N2, NH, VL, PA, CN, DD, AM, PK, CT = [(2, 0), (2, 128), (2, 256), (2, 384), (4, 0), (4, 128), (4, 256), (4, 128),
+                                                           (6, 0), (4, 384), (6, 256), (6, 384), (4, 256)]
+
+    def P(s, lo, hi):
+        if s == SIG:
+            c = 64 * (lo // 128) + lo % 64
+            return V("ps%d" % (2 + lo // 64 % 2), c, c + hi - lo)
+        return V("ps%d" % (s[0] + lo // 128), s[1] + lo % 128, s[1] + lo % 128 + hi - lo)
+
+    def sel(m, k):
+        return V(m, 15 - k, 143 - k)
+
+    load("s", V("X", 0, 4096), "lit", 6000)
+    load("a", V("pci", 0, 256), "pn", 2200)
+    load("a", V("pci", 256, 512), "cn", 2400)
+    load("s", V("wi"), "wt", 2500)
+    load("s", V("ti", p1=8), "th", 2500)
+    load("s", V("NN", 0, 256), "neg", 3000)
+    iota(V("pi", 0, 1), [[0, 1]], 1)
+    iota(V("Ja"), [[1, 16], [0, 2]], 0)
+    iota(V("Mi"), [[1, 144]], 0)
+    iota(V("Mg"), [[16, 8], [0, 16]], 0)
+    Jh = V("Ja", 0, 32, 2)
+    ts(V("pi", 1, 2), V("pi", 0, 1), 15, A.bitwise_and)
+    ts(V("pi", 2, 3), V("pi", 0, 1), 31, A.bitwise_and)
+    cp(V("col", 0, 3), V("pi", 0, 3))
+    ts(col(3), col(1), 16.0, A.mult)
+    ts(V("oA"), V("Ja"), col(3), A.add)
+    ts(V("oB"), Jh, 32.0, A.mult, col(2), A.add)
+    for j, nm in enumerate(("pf", "CF")):
+        a, b = V("t1", 512 * j, 512 * j + 512), V("t2", 512 * j, 512 * j + 512)
+        cp(a, IND(V("pci", 256 * j, 256 * j + 256), V("oA")))
+        tr(b, a)
+        act(V(nm, 0, 256), IND(b, V("oB")), F.Copy)
+    act(V("nz", 0, 1), col(1), F.Sigmoid, -128.0, 256.0, extra=1300.0)
+    ts(col(4), col(0), col(1), A.subtract, 15.0, A.add)
+    ts(col(5), col(0), 1.0, A.add)
+    ts(col(6), col(1), 15.0, A.not_equal)
+    ts(col(7), col(1), 0.0, A.is_equal)
+    ts(col(8), col(7), 2304.0, A.mult, -2176.0, A.add)
+    ts(col(9), col(1), 1.0, A.is_equal, 8191.0, A.mult)
+    tt(col(10), col(9), V("nz", 0, 1), A.add)
+    ts(col(11), V("wi"), 0.0625, A.mult)
+    ts(col(12), col(1), 15.0 / 32, A.add)
+    ts(col(13), col(1), 31.0, A.mult, col(2), A.add)
+    ts(col(14), col(0), 16.0, A.mult)
+    ts(V("oC"), V("Ja"), 16.0, A.mult, col(1), A.add)
+    ts(V("oD"), Jh, col(13), A.add)
+    ts(V("b16"), Jh, 256.0, A.mult, col(3), A.add)
+    ts(V("bi"), Jh, 16.0, A.mult, col(12), A.add)
+    ms(V("X", 4096, 4112), -255.0)
+    ms(V("Rs"), 0.0)
+    ms(V("Rs", 0, 2048, 16), 255.0)
+    mwo, o = [], 0
+    for b, n in enumerate(BC):
+        ms(V("Mw", 16 * (o + b), 16 * (o + b) + 16), 255.0)
+        mwo += [16 * (b + 1)] * n
+        o += n
+    Mi = V("Mi", 0, 128)
+    ts(V("SZ"), V("Mi"), col(4), A.is_equal)
+    ts(V("SH"), V("SZ"), -4096.0, A.mult)
+    ts(V("S8"), V("SZ"), 8192.0, A.mult)
+    ts(col(15), col(4), -15.0, A.add)
+    ts(col(16), col(1), 0.0, A.not_equal)
+    for j, (s, w) in enumerate((("1", col(16)), ("2", col(10)), ("W", col(11)))):
+        if j in cfg["PS"]:
+            ts(V("K" + s), V("Mg"), col(15), A.is_equal, w, A.mult)
+        else:
+            ts(V("S" + s), V("SZ"), w, A.mult)
+    if cfg["PS"]:
+        iota(V("Ml"), [[0, 8], [1, 16]], 0)
+        ts(V("Cz"), V("Ml"), col(1), A.not_equal, -32768.0, A.mult)
+        ts(V("Cb"), Mi, 16.0, A.mult)
+        tt(V("Cb"), V("Cb"), V("Cz"), A.add)
+        ts(V("R0"), V("Ml"), 0.0, A.not_equal)
+    ts(V("Ib"), Mi, col(0), A.is_equal)
+    ts(V("In"), V("Ib"), -1.0, A.mult)
+    ts(V("Ih"), V("Ib"), 0.5, A.mult)
+    ts(V("En"), V("Mg"), col(0), A.is_equal, -1.0, A.mult)
+    ts(V("Ep"), V("En"), -256.0, A.mult)
+    ts(V("Em"), V("En"), 256.0, A.mult)
+    tt(V("Am"), V("Ib"), V("En"), A.add)
+    act(V("If"), V("Ib"), F.Copy)
+    ts(V("Dt"), Mi, col(5), A.is_equal, col(6), A.mult)
+    ts(V("Dm"), V("Ib"), V("nz", 0, 1), A.mult)
+    tt(V("Dm"), V("Dt"), V("Dm"), A.subtract)
+    tt(V("Wm"), V("Ib"), sel("SZ", 0), A.subtract)
+    tt(V("DW"), V("Dm"), sel("SZ", 1), A.subtract)
+    ts(V("Sa"), Mi, 0.0, A.mult, col(7), A.add)
+    ts(V("G8", p1=8), V("Mg", p1=8), V("col", 14, 15, p1=8), A.is_equal)
+    cp(V("tf", 0, 1, p1=8), V("ti", p1=8))
+    mm([(V("ps7", 320, 321), V("G8", p1=8), V("tf", 0, 1, p1=8))])
+    ts(V("tf", 1, 2), V("ps7", 320, 321), 0.0, A.add)
+    ts(V("bz", 0, 1), V("ps7", 320, 321), -4096.0, A.mult)
+    act(V("Td"), V("If"), F.Identity, 0.0, V("bz", 0, 1))
+    ms(V("on"), 1.0)
+
+    def chunks(c, o=0):
+        out = []
+        for n in c:
+            out.append((o, o + n))
+            o += n
+        return out
+
+    def p_forms(lo, hi):
+        cp(V("pu", lo, hi), V("pf", lo, hi))
+        act(V("pp", lo, hi), V("pf", lo, hi), F.Identity, 1184.0)
+        act(P(UP, lo, hi), V("pf", lo, hi), F.Identity, -2555904.0, 2080.0)
+
+    def turn_out(j, src, name):
+        a, b = V("t1", 512 * j, 512 * j + 512), V("t2", 512 * j, 512 * j + 512)
+        act(a, IND(src, V("oC")), F.Copy)
+        tr(b, a)
+        y = V("yo", 256 * j, 256 * j + 256)
+        cp(y, IND(b, V("oD")))
+        store("s", name, 0, 256, y, 2300)
+
+    for lo, hi in chunks(BC):
+        p_forms(lo, hi)
+    Xw = V("X")
+    for t in range(RO):
+        c0 = 256 * t
+        now[:] = ["", set()]
+        for lo, hi in chunks(HC):
+            cf = V("CF", c0 + lo, c0 + hi)
+            grp[0] = "h%d" % lo
+            cp(V("cu", lo, hi), cf)
+            act(P(CT, lo, hi), cf, F.Identity, -2048.0)
+            tt(V("tq", lo, hi), P(CT, lo, hi), V("pp", lo, hi), A.mult)
+            tt(V("vi", lo, hi), P(UP, lo, hi), V("tq", lo, hi), A.add)
+            ts(V("hi", lo, hi), V("vi", lo, hi), 5, A.arith_shift_right, 4095, A.bitwise_and)
+        for j, (lo, hi) in enumerate(chunks(FC)):
+            r0, r1 = 16 * lo, 16 * hi
+            grp[0] = "f%d" % lo
+            for nm, ix, onv in (("xb", "pu", cfg["XV"]), ("yb", "cu", cfg["YV"])):
+                for a, b in chunks(cfg["GS"].get(j, [hi - lo]) if nm == "xb" or j in cfg["MXP"] else [hi - lo], lo):
+                    if j in onv:
+                        cp(V(nm, 16 * a, 16 * b), IND(Xw, V(ix, a, b)))
+                    else:
+                        act(V(nm, 16 * a, 16 * b), IND(Xw, V(ix, a, b)), F.Copy)
+            for a, b in chunks(cfg["GS"].get(j, [hi - lo]), lo):
+                y = V("yb", 16 * a, 16 * b) if j in cfg["MXP"] else IND(Xw, V("cu", a, b))
+                tt(V("mx", 16 * a, 16 * b), y, V("xb", 16 * a, 16 * b), A.max)
+            tok = "k%d" % (lo // 64 % 2)
+            for u, (s, b) in enumerate((("SH", "xb"), ("SH", "yb"), ("S8", "mx"))):
+                mm([(P(SIG, lo, hi), V("Td"), V("on", 0, hi - lo))] * (u == 0)
+                   + [(P(SIG, lo, hi), sel(s, k), V(b, r0 + k, r1, 16)) for k in range(16)], u == 0, u == 2, tok)
+            tt(V("a1", lo, hi), P(SIG, lo, hi), V("hi", lo, hi), A.max)
+            ts(V("hu", lo, hi), V("a1", lo, hi), 4096.0, A.min)
+            for a, b in chunks(cfg["LS"].get(j, [hi - lo]), lo):
+                z, a, b = IND(Xw, V("hu", a, b)), 16 * a, 16 * b
+                if j in cfg["ZA"]:
+                    act(V("zb", a, b), z, F.Copy)
+                    z = V("zb", a, b)
+                tt(V("lp", a, b), z, V("mx", a, b), A.min)
+                act(V("la", a, b), V("lp", a, b), F.Abs)
+                scan(V("Mw", mwo[lo] + a, mwo[lo] + b), V("Rs", 0, b - a), V("la", a, b))
+            for e0 in range(lo, hi, 64):
+                e1 = min(hi, e0 + 64)
+                w = 8 * (e1 - e0)
+                for par in range(2):
+                    bk = "ps%d" % par
+                    mo = mwo[lo] + 16 * e0
+                    mm([(V(bk, 0, w), V("Ib"), V("Mw", mo + par, mo + 2 * w, 2))]
+                       + [(V(bk, k, w, 8), V("In"), V("NN", c0 + e0, c0 + e1)) for k in range(8)])
+                    act(V("Bb", 1 + 16 * e0 + par, 1 + 16 * e1, 2), V(bk, 0, w), F.Sigmoid, 128.0, 256.0)
+            mm([(P(CN, lo, hi), sel("SZ", (k + 1) % 16), V("Bb", 1 + r0 + k, 1 + r1, 16)) for k in range(16)])
+        for b, (lo, hi) in enumerate(chunks(BC)):
+            r0, r1, h0, h1 = 16 * lo, 16 * hi, lo // 16, hi // 16
+            nh_ = h1 - h0
+            grp[0] = "b%d" % lo
+            n_, cf = V("NN", c0 + lo, c0 + hi), V("CF", c0 + lo, c0 + hi)
+
+            def L(name):
+                return V(name, lo, hi)
+
+            def picks(j, s, src, base):
+                if j not in cfg["PS"]:
+                    o = P(PK, lo, lo + nh_)
+                    mm(([(o, V("Ib"), V("b16", 0, nh_))] if base else []) + [(o, sel("S" + s, il), V(src, lo + il, hi, 16)) for il in range(16)])
+                    return o
+                mm([(P(PK, lo, hi), V("Ib"), V("Cb" if base else "Cz", 0, hi - lo)), (P(PK, lo, hi), V("K" + s), L(src))])
+                add("v", "scan2", (L("pk"), V("R0", 0, hi - lo), P(PK, lo, hi)), [L("pk")], [V("R0", 0, hi - lo), P(PK, lo, hi)], ("c", hi - lo))
+                return V("pk", lo + 15, hi, 16)
+
+            tok = "n%d" % (lo // 128)
+            act(P(ZC, lo, hi), L("a1"), F.Identity, 4096.0 * 4096.0, -4096.0)
+            tt(P(ZC, lo, hi), P(ZC, lo, hi), L("pf"), A.max)
+            tt(L("Nf"), P(ZC, lo, hi), L("a1"), A.min)
+            mm([(P(DD, lo, hi), V("Dm"), L("Nf"))], tok=tok)
+            act(L("Ds"), P(DD, lo, hi), F.Copy)
+            act(L("nb"), P(CN, lo, hi), F.Sigmoid, -2176.0, 256.0, acc=V("acc", b, b + 1) if t < RO - 1 else None)
+            o = picks(0, "1", "nb", True)
+            cp(V("i1", h0, h1), o)
+            law = IND(V("la", r0, r1), V("i1", h0, h1))
+            act(L("lk"), law, F.Copy)
+            if b in cfg["CA"]:
+                mm([(P(PK, lo, hi), V("In"), n_), (P(PK, lo, hi), V("Ib"), L("lk"))])
+                act(V("Bb", r0, r1, 16), P(PK, lo, hi), F.Sigmoid, 128.0, 256.0)
+            else:
+                tt(V("Bb", r0, r1, 16), law, n_, A.is_ge)
+            scan(V("B2", r0, r1), V("Rs", 0, r1 - r0), V("Bb", r0, r1))
+            mm([(P(CN, lo, hi), sel("SZ", j + 1), V("B2", r0 + j, r1, 16)) for j in range(15)])
+            mm([(P(AM, lo, hi), V("Am"), L("nb"))])
+            tt(L("ta"), P(AM, lo, hi), L("Ds"), A.mult)
+            if cfg["DA"]:
+                mm([(P(DD, lo, hi), V("DW"), L("ta"))], tok=tok)
+                tt(L("Ds"), P(DD, lo, hi), L("Ds"), A.add)
+            else:
+                mm([(P(DD, lo, hi), V("Dm"), L("Nf")), (P(DD, lo, hi), V("DW"), L("ta"))], tok=tok)
+                act(L("Ds"), P(DD, lo, hi), F.Copy)
+            mm([(P(NH, lo, hi), V("Ib"), n_), (P(NH, lo, hi), V("Ep"), L("nb"))], tok=tok)
+            act(L("nh"), P(NH, lo, hi), F.Identity, -256.0)
+            mm([(P(N2, lo, hi), V("If"), L("Nf")), (P(N2, lo, hi), V("Wm"), L("ta"))], True, False, tok)
+            act(L("kp"), P(CN, lo, hi), F.Sigmoid, col(8), 256.0)
+            mm([(P(AM, lo, hi), V("En"), L("nb")), (P(AM, lo, hi), V("Ib"), L("kp"))])
+            tt(L("tb"), P(AM, lo, hi), L("Ds"), A.mult)
+            mm([(P(N2, lo, hi), V("Wm"), L("tb"))], False, True, tok)
+            o = picks(1, "2", "kp", True)
+            ts(V("i2", h0, h1), o, 16.0 - 8192.0, A.add, 0.0, A.max)
+            m0 = 16 * (lo + b)
+            tt(L("Mm"), IND(V("Mw", m0, m0 + 16 + r1 - r0), V("i2", h0, h1)), L("lk"), A.min)
+            o = picks(2, "W", "Mm", False)
+            tt(V("qq", h0, h1), o, V("bi", 0, nh_), A.subtract)
+            tt(V("ff", h0, h1), o, V("qq", h0, h1), A.subtract)
+            ts(V("i3", h0, h1), V("ff", h0, h1), 16.0, A.mult)
+            mm([(P(VL, lo, hi), V("Ih"), n_), (P(VL, lo, hi), V("Ih"), L("Mm"))], tok=tok)
+            if b in cfg["VA"]:
+                act(L("vf"), P(VL, lo, hi), F.Identity, 12582912.0, 1.0 - 2.0 ** -10)
+                act(L("vb"), L("vf"), F.Identity, -12582912.0)
+                cp(IND(V("X", r0, r1), V("i3", h0, h1)), L("vb"))
+            else:
+                ts(L("vl"), P(VL, lo, hi), -0.25, A.add)
+                cp(IND(V("X", r0, r1), V("i3", h0, h1)), L("vl"))
+            sm = V("SM", c0 + lo, c0 + hi)
+            if b in cfg["SA"]:
+                mm([(P(PA, lo, hi), V("Em"), L("nb")), (P(PA, lo, hi), V("In"), L("nh")), (P(PA, lo, hi), V("Ib"), L("Mm"))], tok=tok)
+                act(L("vf"), P(PA, lo, hi), F.Relu)
+                mm([(P(PA, lo, hi), V("Ib"), L("nh")), (P(PA, lo, hi), V("If"), L("vf"))], tok=tok)
+                act(sm, P(PA, lo, hi), F.Copy)
+            else:
+                mm([(P(PA, lo, hi), V("Em"), L("nb")), (P(PA, lo, hi), V("Ib"), L("Mm"))], tok=tok)
+                tt(sm, P(PA, lo, hi), L("nh"), A.max)
+            send(V("NN", c0 + 256 + lo, c0 + 256 + hi), sm, t)
+            sc = V("SC", c0 + lo, c0 + hi)
+            act(sc, P(N2, lo, hi), F.Copy)
+            send(V("CF", c0 + 256 + lo, c0 + 256 + hi), sc, t)
+            tt(P(QR, lo, hi), P(N2, lo, hi), cf, A.subtract)
+            tt(P(QR, lo, hi), P(QR, lo, hi), L("kp"), A.mult)
+            tt(L("pf"), P(QR, lo, hi), cf, A.add)
+            if t < RO - 1:
+                p_forms(lo, hi)
+            else:
+                store("s", "yx", r0, r1, V("X", r0, r1), 1800 + 4200 * (hi - lo) // NL)
+        if t < RO - 1:
+            o = V("ps7", 128, 129)
+            mm([(o, V("Sa"), V("acc", b, b + 1)) for b in range(len(BC))])
+            cp(V("ai", 0, 1), o)
+            ts(V("ai", 1, 2), V("ai", 0, 1), 63, A.bitwise_and)
+            ts(V("bz", 0, 1), V("ai", 1, 2), V("tf", 1, 2), A.add, -4096.0, A.mult)
+            act(V("Td"), V("If"), F.Identity, 0.0, V("bz", 0, 1))
+    now[:] = ["e", set()]
+    turn_out(0, V("pf"), "yp")
+    turn_out(1, V("CF", 256 * RO, 256 * RO + 256), "yc")
+    store("a", "yn", 0, 256, V("NN", 256 * RO, 256 * RO + 256), 2200)
+
+    seen = {}
+    for i, o in enumerate(ops):
+        dep = set()
+        for kind, lst in (("r", o["r"]), ("w", o["w"])):
+            for nm, a, b in lst:
+                for (j, k2, c, d) in seen.get(nm, ()):
+                    if c < b and a < d and (kind == "w" or k2 == "w"):
+                        dep.add(j)
+        for nm, a, b in o["w"]:
+            seen[nm] = [e for e in seen.get(nm, ()) if not (a <= e[2] and e[3] <= b and o["kind"] != "x")] + [(i, "w", a, b)]
+        for nm, a, b in o["r"]:
+            seen.setdefault(nm, []).append((i, "r", a, b))
+        dep.discard(i)
+        o["dep"] = dep
+        o["banks"] = sorted(set(nm for nm, a, b in o["r"] + o["w"] if nm.startswith("ps")))
+    return ops
+
+
+def times(o, C):
+    k, n = o["n"]
+    if k == "dma":
+        return 100.0, float(n)
+    if k == "rem":
+        return 400.0, C["rem"]
+    if k == "pe":
+        d = n * C["pe"] + C["fp"] * o["cnt"]
+        return d, d + 60.0
+    f = C["fa"] if o["eng"] == "a" else C["fv"]
+    per = {"G": C["G"], "S": C["S"], "tt2": C["tt2"], "c": 1.0}[k]
+    d = f + max(n * per, 30.0) * C["cyc"] + o.get("extra", 0.0)
+    return d, d
+
+
+def run(ops, C, order=None, prio=PRIO, passes=6):
+    n = len(ops)
+    tm = [times(o, C) for o in ops]
+    free, bank, fin, out = {}, {}, [0.0] * n, []
+
+    def start(i):
+        o = ops[i]
+        s = free.get(o["eng"], 0.0)
+        for j in o["dep"]:
+            s = max(s, fin[j] + C["hop"])
+        for b in o["banks"]:
+            for e, f in bank.get(b, {}).items():
+                if e != o["eng"]:
+                    s = max(s, f + C["hop"])
+        return s
+
+    def place(i, s):
+        o = ops[i]
+        free[o["eng"]] = s + tm[i][0]
+        fin[i] = s + tm[i][1]
+        for b in o["banks"]:
+            bank.setdefault(b, {})[o["eng"]] = fin[i]
+        out.append(i)
+
+    if order is not None:
+        for i in order:
+            place(i, start(i))
+        return out, max(fin), fin
+    succ = [[] for _ in ops]
+    for i, o in enumerate(ops):
+        for j in o["dep"]:
+            succ[j].append(i)
+    pred = [sorted(o["dep"]) for o in ops]
+    hop = C["hop"]
+
+    def sgs(pri, pre, suc, back):
+        busy, st, en = {}, [0.0] * n, [0.0] * n
+        left = [len(x) for x in pre]
+        ready = [i for i in range(n) if left[i] == 0]
+        while ready:
+            i = max(ready, key=lambda j: pri[j])
+            ready.remove(i)
+            o = ops[i]
+            d0, d1 = tm[i]
+            lead = d1 - d0 if back else 0.0
+            s = max([en[j] + hop for j in pre[i]] + [0.0])
+            res = [(o["eng"], lead, d0, 0.0)] + [(b, 0.0, d1, hop) for b in o["banks"]]
+            moved = True
+            while moved:
+                moved = False
+                for r, a, d, gap in res:
+                    lst = busy.setdefault(r, [])
+                    u = len(lst)
+                    while u and lst[u - 1][1] + gap > s + a:
+                        u -= 1
+                    for x, y, e in lst[u:]:
+                        if (gap == 0.0 or e != o["eng"]) and x - gap < s + a + d and s + a < y + gap:
+                            s = y + gap - a
+                            moved = True
+            for r, a, d, gap in res:
+                lst = busy[r]
+                u = len(lst)
+                while u and lst[u - 1][1] > s + a + d:
+                    u -= 1
+                lst.insert(u, (s + a, s + a + d, o["eng"]))
+            st[i], en[i] = s, s + d1
+            for j in suc[i]:
+                left[j] -= 1
+                if left[j] == 0:
+                    ready.append(j)
+        return st, en
+
+    pr = [0.0] * n
+    for i in range(n - 1, -1, -1):
+        pr[i] = tm[i][1] + hop + max([pr[j] for j in succ[i]] + [0.0])
+    pr = [pr[i] + prio.get(ops[i]["key"], 0.0) for i in range(n)]
+    best = None
+    for _ in range(passes):
+        st, en = sgs(pr, pred, succ, False)
+        order = sorted(range(n), key=lambda i: (st[i], i))
+        res = run(ops, C, order)
+        if best is None or res[1] < best[1]:
+            best = res
+        if passes > 1:
+            pr = sgs(res[2], succ, pred, True)[1]
+    return best
+
+
+def waits(ops, order):
+    csem = {"v": "cv", "a": "ca", "p": "cp", "g": "cg"}
+    cnt, known, mark, clock, lastb, out = {}, {}, {}, {}, {}, {}
+    for i in order:
+        o = ops[i]
+        dep = set(o["dep"])
+        for b in o["banks"]:
+            for e, j in lastb.get(b, {}).items():
+                if e != o["eng"]:
+                    dep.add(j)
+        kn = known.setdefault(o["eng"], {})
+        ws = []
+        for j in sorted(dep, key=lambda j: -mark[j][2]):
+            s, c = mark[j][0], mark[j][1]
+            if kn.get(s, 0) >= c:
+                continue
+            ws.append((s, c))
+            kn[s] = c
+            for s2, c2 in clock[j].items():
+                if kn.get(s2, 0) < c2:
+                    kn[s2] = c2
+        out[i] = ws
+        if "sem" in o:
+            mark[i] = (o["sem"], 16, len(mark))
+        else:
+            s = csem[o["eng"]]
+            cnt[s] = cnt.get(s, 0) + 1
+            mark[i] = (s, cnt[s], len(mark))
+        clock[i] = dict(kn)
+        for b in o["banks"]:
+            lastb.setdefault(b, {})[o["eng"]] = i
+    return out, mark, cnt
+
+
+PLAN = {}
+
+
+def plan():
+    if not PLAN:
+        ops = build(CFG)
+        keys = list(dict.fromkeys(o["key"] for o in ops))
+        prio = {k: 100.0 * (int(PR[2 * i:2 * i + 2], 36) - 648) for i, k in enumerate(keys) if 2 * i < len(PR)}
+        order = run(ops, COST, prio=prio, passes=1)[0]
+        PLAN["p"] = (ops, order) + waits(ops, order)
+    return PLAN["p"]
+
+
+def emit(o, ws, mark, g, core, T, topo):
+    q = {"v": g.vector, "a": g.scalar, "p": g.tensor, "g": g, "s": g.sync}[o["eng"]]
+    rank = T.rank_of(core)
+    n = len(T.cores)
+    for s, c in ws:
+        q.wait_ge(T.sem[s], c)
+    k, a = o["kind"], [ap(T, x) for x in o["args"]]
+    if k == "cp":
+        ins = q.tensor_copy(a[0], a[1])
+    elif k == "tt":
+        ins = q.tensor_tensor(a[0], a[1], a[2], a[3])
+    elif k == "ts":
+        ins = q.tensor_scalar(a[0], a[1], a[2], None, a[4]) if a[5] is None else q.tensor_scalar(a[0], a[1], a[2], a[3], a[4], a[5])
+    elif k == "scan":
+        ins = q.tensor_tensor_scan(a[0], a[1], a[2], 0.0, A.max, A.min)
+    elif k == "scan2":
+        ins = q.tensor_tensor_scan(a[0], a[1], a[2], 0.0, A.mult, A.max)
+    elif k == "ms":
+        ins = q.memset(a[0], a[1])
+    elif k == "tr":
+        ins = q.transpose(a[0], a[1])
+    elif k == "act":
+        if a[2] in (F.Copy, F.Abs, F.Relu):
+            ins = q.activation(a[0], a[1], a[2])
+        elif a[5] is None:
+            ins = q.activation(a[0], a[1], a[2], bias=a[3], scale=a[4])
+        else:
+            ins = q.activation(a[0], a[1], a[2], bias=a[3], scale=a[4], accum_out=a[5])
+    elif k == "mm":
+        for j, m in enumerate(a):
+            ins = q.matmul(ap(T, m[0]), ap(T, m[1]), ap(T, m[2]), j == 0 and o["start"], j == len(a) - 1 and o["stop"])
+    elif k == "iota":
+        if SCRATCH[o["args"][0]["name"]][2] == I32:
+            ins = q.iota(a[0], a[1], 0, a[2])
+        else:
+            ins = q.iota(a[0], a[1], 0, a[2], allow_small_or_imprecise_dtypes=True)
+    elif k == "load":
+        ins = q.dma_start(a[0], T[a[1]][:])
+    elif k == "store":
+        ins = q.dma_start(T[a[0]][:, a[1]:a[2]], a[3])
+    else:
+        dst = T.cores[(rank + 1 + a[2] % 3) % n]
+        rid, pid, _ = topo.addr(dst)
+        q.remote_dma(a[0], a[1], T.sem[o["sem"]], T.sem["loc"], pid, rid, topo.mask(core, dst))
+        return len(topo.engines(core, dst))
+    ins.then_inc(T.sem[mark[0]], 16 if "sem" in o else 1)
+    return 0
+
+
+def rank_program(g, core, T, topo):
+    if T.rank_of(core) is None:
+        return
+    ops, order, ws, mark, cnt = plan()
+    loc = 0
+    for i in order:
+        loc += emit(ops[i], ws[i], mark[i], g, core, T, topo)
+    for s, c in cnt.items():
+        g.wait_ge(T.sem[s], c)
+    g.wait_ge(T.sem["loc"], loc)
+    for o in ops:
+        if o.get("last"):
+            g.wait_ge(T.sem[o["sem"]], 16)

@@ -2,10 +2,13 @@ import numpy as np
 from concourse.mybir import AluOpType as A, ActivationFunctionType as F
 
 RO, NL = 5, 256
-CFG = dict(FC=[64, 64, 64, 64], BC=[128, 128], HC=[128, 128], XV=(1,), YV=(), MXP=(), ZA=(), PS=(0, 1, 2), DA=False,
+CFG = dict(FC=[64, 64, 64, 64], BC=[128, 128], HC=[128, 128], XV=(1,), YV=(), MXP=(1, 2, 3), ZA=(), PS=(0, 1, 2), DA=False,
            GS={0: [16, 48]}, LS={3: [32, 32]}, CA=(), VA=(0,), SA=(0, 1))
 PRIO = {}
 PR = "jzj8jfk8hgiqlkiymdkpkgizjvn1nvl8khlpk2k0jxgyhdjdl3ksiqihhxhfjnkajnkdjlktkfkojujvlnksl5kxk0jll6l6kckpkknah8hxiaiynekdh5kdjglxmajfjyjaiqkohlh2gbhhjhmhnniulalfkulohij5jmkei2jfhhhohdhhhahhh5ighjiniflqmumqmpishxi1jfkulxlnlyl1kqnio2hrisi7i1h9hvjxichqhyhxhyi0hdkzkxixhsj2jak5kgk3m5kthvl8icjuh2hrhlhvh1icjwk4jojfh5h4hkh8hoiahzhyi1h5i9hvjzi5iyiihoigighzi3ijjajaich4hjifjhj9hzhxjhirjojbhiijifhvhtiziyjbkekekcg9gqk9iokrj9i1mzobsco3mdl8l2lvhckrj3j3l7jkigguiuitjpj7haiehaimhlitghk1kll1kdhtjej2jii9ithdifhhhojijyh7h4i2hcidjjiljli8i6jdhhhkh3ibibgaiihpiwfxi9hpefengcglg6"
+PR = "kdpupplwiflhmpkqnilhh8h8gymuo0l1kalwpkkooxo0p4mlkgjzjplbjhjflnl9j5juidh8j2ijhiiti8khl4kzllj4hdjqn0nimxq5i0jhjgjeq7nci7ilkjmxmmpdmsmdi6khhbgsgbheh9jsl5nrilh5njn5gznyppkaipjti4i3h6h3h5hfhqk6ixjljsnhnznhnfhui4i5jjl3l3lrlknfn4pqqskhlel5kzhrhwlqjbhui9ilicj4ielmlkjkimjuk1ktmekonulhinn6j4kah3idhyi9gjhzk3lwlekmibizl4ipjcjajhj6jni2jai4kxiaiui8hnjiilh7ixjdjhj1iyk9hgilisj0hkjfk1icj1kpgrj9iehoiukjlcl5lzm2ohi4hdm1j1nglbi8qdrdurqiljl2n5mmhtlckbkim3lpiui9lwlvmpmyjqkwibhiiti0hsmxn3njn5m9msl0lkhuh5hdizhwi9kekuk5jrm4j3jpkjjnklhwimj4iciuigjbjei4ihhtk5gaijiffoeygngyhf"
+CFG.update(SA=(), VA=(), XV=(), YV=(0,), MXP=(0, 1, 2, 3))
+PR = "irm8ldnjnrmrmvmqn4n7lzk6jtjzljjvkfkkj4llo8m5lom8n5m4p2tqqbs7pflhnho6lvlempn5n9l0lin4mdogplr6szr0rwtqrdq8nam2hujfjmnlovjihxi3hvkojzl1jkjricjgk1kllckwm9m0kqmpmulzlklil8j7juimi3kdn8kol1kckvlnlblakrjzjmlhlhjok1j3iciohpjdioioiviyk7l1j4j0idhlh7hlhljci1i1jyi7jejyitibhxi3hchxi1hnjrhvhvhshuhshuhthzi5hzhphmhjhkifhzhwijhqhwhohpgwhlgrhxjejfioi3j6igikk6ihi5i4i6icijili4hxj0goi1i4iekyjfjsjdidkajjjhi9hni4hmi3ihi6ioiajdiii3itj2j3jmijikkripholdk1ikjaj1j4iuiuicj1h2hwiehdhxhqifh7hnhphnifioj2i5jdhxhlhphvhyhmhxh4hqhsnjn7hohti5ijk7k2jahylhj0hsj2gefogafffggxk7kgm7"
 BF, F32, I32, U16 = "bfloat16", "float32", "int32", "uint16"
 
 

@@ -1,14 +1,14 @@
 import numpy as np
+from concourse.bass import DstId, RemoteDMATransfer
 from concourse.mybir import AluOpType as A, ActivationFunctionType as F
 
 RO, NL = 5, 256
-CFG = dict(FC=[64, 64, 64, 64], BC=[128, 128], HC=[128, 128], XV=(1,), YV=(), MXP=(1, 2, 3), ZA=(), PS=(0, 1, 2), DA=False,
-           GS={0: [16, 48]}, LS={3: [32, 32]}, CA=(), VA=(0,), SA=(0, 1))
-PRIO = {}
-PR = "jzj8jfk8hgiqlkiymdkpkgizjvn1nvl8khlpk2k0jxgyhdjdl3ksiqihhxhfjnkajnkdjlktkfkojujvlnksl5kxk0jll6l6kckpkknah8hxiaiynekdh5kdjglxmajfjyjaiqkohlh2gbhhjhmhnniulalfkulohij5jmkei2jfhhhohdhhhahhh5ighjiniflqmumqmpishxi1jfkulxlnlyl1kqnio2hrisi7i1h9hvjxichqhyhxhyi0hdkzkxixhsj2jak5kgk3m5kthvl8icjuh2hrhlhvh1icjwk4jojfh5h4hkh8hoiahzhyi1h5i9hvjzi5iyiihoigighzi3ijjajaich4hjifjhj9hzhxjhirjojbhiijifhvhtiziyjbkekekcg9gqk9iokrj9i1mzobsco3mdl8l2lvhckrj3j3l7jkigguiuitjpj7haiehaimhlitghk1kll1kdhtjej2jii9ithdifhhhojijyh7h4i2hcidjjiljli8i6jdhhhkh3ibibgaiihpiwfxi9hpefengcglg6"
-PR = "kdpupplwiflhmpkqnilhh8h8gymuo0l1kalwpkkooxo0p4mlkgjzjplbjhjflnl9j5juidh8j2ijhiiti8khl4kzllj4hdjqn0nimxq5i0jhjgjeq7nci7ilkjmxmmpdmsmdi6khhbgsgbheh9jsl5nrilh5njn5gznyppkaipjti4i3h6h3h5hfhqk6ixjljsnhnznhnfhui4i5jjl3l3lrlknfn4pqqskhlel5kzhrhwlqjbhui9ilicj4ielmlkjkimjuk1ktmekonulhinn6j4kah3idhyi9gjhzk3lwlekmibizl4ipjcjajhj6jni2jai4kxiaiui8hnjiilh7ixjdjhj1iyk9hgilisj0hkjfk1icj1kpgrj9iehoiukjlcl5lzm2ohi4hdm1j1nglbi8qdrdurqiljl2n5mmhtlckbkim3lpiui9lwlvmpmyjqkwibhiiti0hsmxn3njn5m9msl0lkhuh5hdizhwi9kekuk5jrm4j3jpkjjnklhwimj4iciuigjbjei4ihhtk5gaijiffoeygngyhf"
-CFG.update(SA=(), VA=(), XV=(), YV=(0,), MXP=(0, 1, 2, 3))
-PR = "irm8ldnjnrmrmvmqn4n7lzk6jtjzljjvkfkkj4llo8m5lom8n5m4p2tqqbs7pflhnho6lvlempn5n9l0lin4mdogplr6szr0rwtqrdq8nam2hujfjmnlovjihxi3hvkojzl1jkjricjgk1kllckwm9m0kqmpmulzlklil8j7juimi3kdn8kol1kckvlnlblakrjzjmlhlhjok1j3iciohpjdioioiviyk7l1j4j0idhlh7hlhljci1i1jyi7jejyitibhxi3hchxi1hnjrhvhvhshuhshuhthzi5hzhphmhjhkifhzhwijhqhwhohpgwhlgrhxjejfioi3j6igikk6ihi5i4i6icijili4hxj0goi1i4iekyjfjsjdidkajjjhi9hni4hmi3ihi6ioiajdiii3itj2j3jmijikkripholdk1ikjaj1j4iuiuicj1h2hwiehdhxhqifh7hnhphnifioj2i5jdhxhlhphvhyhmhxh4hqhsnjn7hohti5ijk7k2jahylhj0hsj2gefogafffggxk7kgm7"
+CFG = dict(FC=[32, 32, 64, 64, 32, 32], QC=[64, 64, 64, 64], BC=[128, 128], HC=[128, 128], FW=32, XV=(), YV=(), ZA=(3,), ZV=(), FO=(),
+           FV=(), PS=(0, 1, 2), SA=(), SM=(0, 1), UA=True, PE=False, Q2=1, ST=(0, 1, 2, 3), VA=(), MA=())
+ORDER = "sBS768 swi0> pu0< scol24 scol3> soD0 X4< X0< nT0 sWm0 stf0 cu0 u14< C16 scol7 tq0 ta4 K04 scol11 Dn1> Sx1 NN0< sAm0 yx4< Dw0 SM4< sCb0 K00 sSZ0 k10 sRs0+ son0 k24 scol17 tq4 sNN0> ai0< NH0 C26 yb0> Sy0 spu128 A14 hu0> bz0 sd4 spp0> eyn0<< snz0> scol6 xb1 mx0 Sx2 sEn0 cu4 Dn5 xb2 pu4 stf1 mx1 C14 Dn4 sDw0 vi4 lp0 soA0> yb2 lp2 sIb0> sBS384 scol4> eyo0<< nk0 PP4< sBS0 nk1 nk2 xb4 yb4 Sm2 spi1> Bb6 sps50> vl4 u24 eyo256< DA4 Sy4 Dw5 Sx4 Dn2 Dw1 UC4 sG80> yb6 Sx0> sZn0 SC4 Dl2 xb6 mx4 Dn0> w14 B22 hi4 sDw2064 K14 xb7 slp2048 SM0 NN4< Dk3 DK0 yb7 tb0 Sx6 Dw4 vl0 et2512<< Dl3 Sy6 Dw2 Sm4 hu4 tb4 mx6 scol5> OK0 Sx7 hi0> OK4 nk4 sDW0+ spci0> B20 Dw3 Sy7 Dk5 NK0 sEp0 Bb1 Bb0 et20<< sX0> lp1> Dk4 lp6 mx7 C12 eyp0< et1512< Sm7 scol12> sK10 sti0> scol19> lp4 scol15>> lp7 Dl4 Bb2 Dk0> sDt0 sCF0> sDW0++ nk6 ai1 et10< C10 Dl5 nk7 sMg0>> Bb3 Sm1> DK4 spci256> sK20 Dn6 Dn3> sps40> vi0>> sEx0> soB0> Dn7 Dk6 sbi0> scol23 scol20 Dk7 ta0 Sy2> Dl6 NT0> scol16 sDm0> Dl7 nb0 PP0 sZp0> sR00 sEm0 NK4 A10 w20 w10 spi0> Bb4 sBS128> CF0 sIn0 st10> nh4> Sm0> lk0 pp4< DA0 Bb5 scol8 k04 Dw6 scol9 snh0> sSN0> Dw7 slp4112> sBS640> lk4 A24 scol10 k00 w24 C24 sd0 Sm6> D10 i10> i20 scol18 CF4> A20 scol13> sLm0+ nb4 DB0 sTH> C22 sbz0> sIf0 sDg0> yb1> sBS896> K10 sKE0 sKW0 st1512> Dl0>> st20>> C20 soC0> sMi0> B24 Dk1> i14 sIh0 B26 pp0 spi2> D14 st2512> dk0 kp0 Sy1> sMl0> tc4 eyc0< u10 D20 dk4 Bb7> DM0 k14 DB4 kp4 sSa0 sDm0+> yx0 D24 nh0 i24 Na0> Dl1> sLm0> Nb0 spu0> scol0> K20 sDW0> sEx0+> NH4 Na4 DM4 u20 PA0 SC0 sRs0> k20 Nb4 VL4 sJa0>> sCz0> Dk2> qq0 sSD0> sBS512> K24 VL0 qq4 zb4> NT4> AS UC0> mx2> tc0 sGm0> ff4 ff0 i34 scol14> sBS256>> PA4 i30 xb0> nT4>"
+CFG.update(ZA=(3,), YV=(0,), FV=(7,))
+ORDER = "xb1 xb0 ai0< u14< tq0 ai1< cu0 bz1< u24< yb0 UC0 vi0 yb1 Th0< tc4< mx0 hi0 pu4< mx1 hu0 lp0 lp1 xb2 yb2 mx2 cu4 lp2 NT0 Sx0 Sy0 nT0 Sx2 Sm0 NT4 nt0 Dn1 St0 Dn0 Sy2 Sm2 xb4 nk0 Dk0 Dk1 yb6 nt2 yb4 Dl0 Dw0 St2 nk2 Dl1 Dw1 Sx4 Dn2 Sy4 mx4 Dn3 Dk2 Sm4 UC4 PP4< tq4 xb6 mx6 xb7 vi4 hi4 hu4 Dk3 Dl2 Dw2 Sx6 Dl3 Dw3 nT4 yb7 nt4 St4 OK0 Dn4 mx7 Sy6 w10 zb4 lp4 lp6 nk4 Dn5 Sm6 Dk5 NK0 Dk4 Dl5 Dl4 Dw4 Dw5 Bb3 Bb2 C12 Bb0 Bb1 C10 nt6 St6 pp4< et10< et20< eyo0< eyn0< eyp0< et1512< et2512< eyo256< eyc0< nb0 nk6 Bb4 Dn6 Dn7 K00 Dk6 NH0 nh0 Dk7 Dl6 lp7 Dl7 k00 i10 w20 DA0 lk0 Bb5 sd0 Dw6 Dw7 Bb7 D10 A10 ta0 C14 OK4 NK4 Bb6 C16 nb4 B20 C20 w24 B22 K04 w14 k04 i14 sd4 lk4 B24 B26 C22 DK0 kp0 DA4 D14 DK4 K10 A20 A14 dk0 C24 k10 i20 ta4 DB0 D20 C26 dk4 kp4 DM0 K20 k20 tb0 Na0 VL0 qq0 vl0 ff0 K14 k14 i30 i24 DM4 NH4 Nb0 SC0 CF0 u10 DB4 D24 A24 nh4 PA4 K24 X0 yx0 u20 SM4 k24 NN4 tb4 qq4 VL4 PA0 SM0 NN0 Na4 Nb4 SC4 CF4 AS ff4 tc0 pp0 PP0 vl4 i34 pu0 X4 yx4"
+SETUP = "pci0 X0 Rs0 pi0 pi2 pi1 Ml0 lp2048 lp4112 ti0 col0 col6 col14 Cz0 cl21 col9 nz0 col15 col7 col23 col16 col20 col8 col12 col3 col5 col10 cl20 col19 Mg0 G80 Gm0 En0 Em0 Ep0 K10 col4 col18 Ja0 oA0 oC0 t10 oB0 t20 pp0 ps50 ps40 R00 col17 GD0 pci256 t1512 tf0 GN0 Rs0+ t2512 CF0 pu128 pu0 TH ai2 Dw0 NN0 on0 Tm0 ai3 @tq0 Ex0 Ex0+ @cu0 Tm0+ @yb0 Lm0 cl22 cl23 @vi0 BS0 BS0+ Zn0 @mx0 cl24 cl25 Th0 Mi0 Ib0 Dt0 Zp0 SZ0 Am0 Wm0 DW0 In0 Ih0 Zo128 Dm0 Zo0 @lp0 DW0+ @nt2 Dm0+ @Dl0 wi0 col11 @mx7 nh0 @C10 Dg0 Cb0 @St6 K20 @nb0 KW0 @Dn6 If0 @lk0 Sa0 @Bb7 bi0 @nh0 DW0++ @sd4 KE0 @lk4 col13 oD0 @DM0 Dw2064 @K20 Lm0+"
 BF, F32, I32, U16 = "bfloat16", "float32", "int32", "uint16"
 
 
@@ -17,30 +17,32 @@ def sb(n, d):
 
 
 SCRATCH = {
-    "X": sb(4112, BF), "xb": sb(4096, BF), "yb": sb(4096, BF), "mx": sb(4096, BF), "lp": sb(4096, BF), "la": sb(4096, BF),
-    "Mw": sb(4096 + 64, BF), "zb": sb(4096, BF), "Td": sb(128, F32), "on": sb(128, F32), "Bb": sb(4112, BF), "B2": sb(4096, BF), "Rs": sb(2048, BF),
+    "X": sb(4096, BF), "xb": sb(4096, BF), "yb": sb(4096, BF), "zb": sb(4096, BF), "mx": sb(4096, BF), "lp": sb(4096 + 128, BF),
+    "Dw": sb(4096 + 128, BF), "Bb": sb(4112, BF), "B2": sb(4096, BF), "Rs": sb(4096, BF), "Ex": sb(512, BF), "BS": sb(1152, BF),
     "pci": sb(512, I32), "t1": sb(1024, F32), "t2": sb(1024, F32), "yo": sb(512, F32),
     "CF": sb(256 * (RO + 1), F32), "NN": sb(256 * (RO + 1), BF), "SC": sb(256 * RO, F32), "SM": sb(256 * RO, BF),
-    "pf": sb(256, F32), "pp": sb(256, F32), "pu": sb(256, U16), "cu": sb(256, U16), "hu": sb(256, U16),
-    "tq": sb(256, F32), "vi": sb(256, I32), "hi": sb(256, I32), "a1": sb(256, F32), "Nf": sb(256, F32),
-    "Ds": sb(256, F32), "ta": sb(256, F32), "tb": sb(256, F32), "nb": sb(256, BF), "kp": sb(256, BF),
-    "lk": sb(256, BF), "Mm": sb(256, BF), "nh": sb(256, BF), "vl": sb(256, I32),
+    "pp": sb(256, F32), "pu": sb(256, U16), "cu": sb(256, U16), "hu": sb(256, U16),
+    "tq": sb(256, F32), "vi": sb(256, I32), "hi": sb(256, I32), "w1": sb(256, F32), "w2": sb(256, F32), "nk": sb(512, BF), "nt": sb(512, BF), "vf": sb(256, F32), "vb": sb(256, BF), "r1": sb(256, BF), "r2": sb(256, BF),
+    "GN": sb(8, BF), "GD": sb(8, BF), "Th": sb(128, BF), "Tm": sb(128, BF), "cl2": sb(16, F32), "Zo": sb(256, BF),
+    "D1": sb(256, F32), "D2": sb(256, F32), "ta": sb(256, F32), "tb": sb(256, F32), "tc": sb(256, F32), "nb": sb(256, BF), "kp": sb(256, BF),
+    "lk": sb(256, BF), "dk": sb(256, BF), "dp": sb(256, BF), "DM": sb(256, BF), "nh": sb(256, BF), "nT": sb(256, BF), "vl": sb(256, I32),
     "i1": sb(16, U16), "i2": sb(16, U16), "i3": sb(16, U16), "qq": sb(16, I32), "ff": sb(16, F32),
     "acc": sb(8, F32), "ai": sb(4, I32), "bz": sb(4, F32),
-    "wi": sb(1, I32), "ti": sb(1, I32), "tf": sb(4, F32), "pi": sb(4, I32), "col": sb(24, F32), "nz": sb(2, BF),
-    "Mi": sb(144, F32), "Mg": sb(128, F32), "Ja": sb(32, F32),
+    "wi": sb(1, I32), "ti": sb(1, I32), "tf": sb(4, F32), "pi": sb(4, I32), "col": sb(32, F32), "nz": sb(2, BF),
+    "Mi": sb(144, F32), "Mg": sb(128, F32), "Ml": sb(128, F32), "Ja": sb(32, F32),
     "oA": sb(32, U16), "oB": sb(16, U16), "oC": sb(32, U16), "oD": sb(16, U16), "b16": sb(16, BF), "bi": sb(16, F32),
     "Ib": sb(128, BF), "In": sb(128, BF), "Ih": sb(128, BF), "Am": sb(128, BF), "En": sb(128, BF), "Ep": sb(128, BF), "Em": sb(128, BF),
-    "SZ": sb(144, BF), "SH": sb(144, BF), "S8": sb(144, BF), "SW": sb(144, BF), "S1": sb(144, BF), "S2": sb(144, BF),
-    "K1": sb(128, BF), "K2": sb(128, BF), "KW": sb(128, BF), "Cz": sb(128, BF), "Cb": sb(128, BF), "R0": sb(128, F32), "Ml": sb(128, F32),
-    "pk": sb(256, F32), "vf": sb(256, F32), "vb": sb(256, BF),
-    "If": sb(128, F32), "Dm": sb(128, F32), "Dt": sb(128, F32), "Wm": sb(128, F32), "DW": sb(128, F32), "Sa": sb(128, F32), "G8": sb(128, F32),
+    "SZ": sb(144, BF), "SN": sb(144, BF), "SD": sb(144, BF), "SW": sb(144, BF), "S1": sb(144, BF), "S2": sb(144, BF), "SE": sb(144, BF),
+    "K1": sb(128, BF), "K2": sb(128, BF), "KW": sb(128, BF), "KE": sb(128, BF), "Cz": sb(128, BF), "Cb": sb(128, BF), "R0": sb(128, F32),
+    "Gm": sb(128, BF), "Zp": sb(144, BF), "Zn": sb(144, BF), "on": sb(128, BF), "Kp": sb(128, BF), "Ku": sb(128, BF), "pk": sb(256, F32),
+    "If": sb(128, F32), "Nf": sb(128, F32), "Uf": sb(128, F32), "Dm": sb(128, F32), "Lm": sb(128, F32), "Ln": sb(128, F32), "Wm": sb(128, F32),
+    "DW": sb(128, F32), "Dt": sb(128, F32), "Dg": sb(128, F32), "Sa": sb(128, F32), "G8": sb(128, F32),
 }
 for _b in range(8):
     SCRATCH["ps%d" % _b] = ("psum", [128, 512], F32)
-SEMAPHORES = ["cv", "ca", "cp", "cg", "loc"] + ["d%d" % i for i in range(24)] + ["r%d" % i for i in range(8 * RO)]
+SEMAPHORES = ["cv", "ca", "cp", "cg", "loc"] + ["d%d" % i for i in range(24)] + ["r%d" % i for i in range(8 * RO)] + ["f%d" % i for i in range(8)]
 
-COST = dict(G=1.56, S=3.8, tt2=1.0, cyc=0.83 * 1.2, pe=0.42 * 1.2, fv=60.0, fa=70.0, fp=10.0, hop=90.0, rem=2200.0)
+COST = dict(G=1.56, Gop=0.5, S=3.8, tt2=1.0, cyc=0.83, pe=0.42, fv=40.0, fa=50.0, mn=50.0, fp=10.0, hop=120.0, rem=2000.0, fb=2.0)
 
 
 def V(name, c0=0, c1=None, st=1, p0=0, p1=128, off=None):
@@ -89,27 +91,40 @@ def spans(vs):
     return out
 
 
+def chunks(c, o=0):
+    out = []
+    for n in c:
+        out.append((o, o + n))
+        o += n
+    return out
+
+
 def build(cfg):
     ops = []
     FC, BC, HC = cfg["FC"], cfg["BC"], cfg["HC"]
-    now, grp = ["s", set()], ["s"]
+    now = ["s", set(), -1]
 
-    def add(eng, kind, args, outs, ins, n, **kw):
+    def add(eng, kind, args, outs, ins, n, nm=None, **kw):
         w = [(v["name"], v["c0"], v["c1"]) for v in outs]
         r = spans(ins) + [(v["off"]["name"], v["off"]["c0"], v["off"]["c1"]) for v in outs if v["off"] is not None]
-        nm, c = (w or r)[0][:2]
-        key = "%s%s%d" % (now[0], nm, c % 256 if nm in ("CF", "NN", "SC", "SM") else c)
+        if nm is None:
+            nm, c = (w or r)[0][:2]
+            wide = SCRATCH[nm][1][1]
+            if now[0] == "":
+                c = c // 512 if wide >= 4096 else c // 64 if nm in ("nk", "nt") else c // 2 if wide == 16 else c % 256 // 32 if wide >= 256 else c
+            nm = "%s%d" % (nm, c)
+        key = now[0] + nm
         while key in now[1]:
             key += "+"
         now[1].add(key)
-        ops.append(dict(eng=eng, kind=kind, args=args, w=w, r=r, n=n, key=key, grp=grp[0], **kw))
+        ops.append(dict(eng=eng, kind=kind, args=args, w=w, r=r, n=n, key=key, rnd=now[2], **kw))
 
     def vcost(out, ins, tt=False):
         n = width(out)
         if out["off"] is not None:
             return ("S", n)
         if ins and ins[0]["off"] is not None:
-            return ("G", n)
+            return ("Gt" if tt else "G", n)
         allb = two(out) and all(two(v) for v in ins)
         if tt and not any(isps(v) for v in ins):
             return ("tt2", n) if allb else ("c", 2 * n)
@@ -118,11 +133,11 @@ def build(cfg):
     def cp(out, a):
         add("v", "cp", (out, a), [out], [a], vcost(out, [a]))
 
-    def tt(out, a, b, op):
-        add("v", "tt", (out, a, b, op), [out], [a, b], vcost(out, [a, b], True))
+    def tt(out, a, b, op, nm=None):
+        add("v", "tt", (out, a, b, op), [out], [a, b], vcost(out, [a, b], True), nm)
 
-    def ts(out, a, s1, op0, s2=None, op1=None):
-        add("v", "ts", (out, a, s1, s2, op0, op1), [out], [a, s1, s2], vcost(out, [a]))
+    def ts(out, a, s1, op0, s2=None, op1=None, nm=None):
+        add("v", "ts", (out, a, s1, s2, op0, op1), [out], [a, s1, s2], vcost(out, [a]), nm)
 
     def scan(out, d0, d1):
         add("v", "scan", (out, d0, d1), [out], [d0, d1], vcost(out, [d0, d1]))
@@ -133,303 +148,394 @@ def build(cfg):
     def tr(out, a):
         add("v", "tr", (out, a), [out], [a], vcost(out, [a]))
 
-    def act(out, a, f, bias=0.0, scale=1.0, acc=None, extra=0.0):
+    def act(out, a, f, bias=0.0, scale=1.0, acc=None, extra=0.0, nm=None):
         add("a", "act", (out, a, f, bias, scale, acc), [out] + ([acc] if acc else []), [a, bias, scale],
-            ("G" if a["off"] is not None else "c", width(out)), extra=extra)
+            ("G" if a["off"] is not None else "c", width(out)), nm, extra=extra)
 
-    def mm(lst, start=True, stop=True, tok=None):
+    def af(out, a, scale, bias=0.0):
+        act(out, a, F.Identity, bias, scale)
+
+    def mm(nm, lst, start=True, stop=True):
         n = sum(max(64, width(m[0])) * (1 if two(m[2]) else 4) for m in lst)
-        add("p", "mm", lst, [m[0] for m in lst], [m[1] for m in lst] + [m[2] for m in lst], ("pe", n), cnt=len(lst), start=start, stop=stop)
-        if tok is not None:
-            ops[-1]["w"].append((tok, 0, 1))
+        add("p", "mm", lst, [m[0] for m in lst], [m[1] for m in lst] + [m[2] for m in lst], ("pe", n), nm, cnt=len(lst), start=start, stop=stop)
 
-    def iota(out, pat, cm):
-        add("g", "iota", (out, pat, cm), [out], [], ("c", 160 + 2 * width(out)))
+    def iota(out, pat, cm, base=0):
+        add("g", "iota", (out, pat, cm, base), [out], [], ("c", 160 + 2 * width(out)))
+
+    def asel(out, pat, cm):
+        add("g", "asel", (out, pat, cm), [out], [out], ("c", 200 + 2 * width(out)))
 
     nd = [0, 0]
 
-    def load(q, out, name, us):
-        add(q, "load", (out, name), [out], [], ("dma", us), sem="d%d" % nd[0])
+    def load(q, out, name, c0, c1, ns):
+        add(q, "load", (out, name, c0, c1), [out], [], ("dma", ns), sem="d%d" % nd[0])
         nd[0] += 1
 
-    def store(q, name, c0, c1, a, us):
-        add(q, "store", (name, c0, c1, a), [], [a], ("dma", us), sem="d%d" % nd[0], last=True)
+    def store(q, name, c0, c1, a, ns):
+        add(q, "store", (name, c0, c1, a), [], [a], ("dma", ns), "%s%d" % (name, c0 // 512), sem="d%d" % nd[0], last=True)
         nd[0] += 1
 
     def send(dst, src, t):
-        add("g", "send", (dst, src, t), [dst], [src], ("rem", 0), sem="r%d" % nd[1])
+        add("g", "send", (dst, src, t), [dst], [src], ("rem", 0), sem="r%d" % nd[1], cum=1)
         nd[1] += 1
 
     def col(j):
         return V("col", j, j + 1)
 
-    SIG, ZC, QR, UP, N2, NH, VL, PA, CN, DD, AM, PK, CT = [(2, 0), (2, 128), (2, 256), (2, 384), (4, 0), (4, 128), (4, 256), (4, 128),
-                                                           (6, 0), (4, 384), (6, 256), (6, 384), (4, 256)]
+    OKP, N2, NKP, UC, PP, NH, VL, EE, DD, CN, AM, PK, MS = [(2, 256), (2, 256), (2, 384), (2, 384), (4, 0), (4, 128), (4, 128), (4, 256),
+                                                            (4, 384), (6, 0), (6, 128), (6, 256), (6, 384)]
 
     def P(s, lo, hi):
-        if s == SIG:
-            c = 64 * (lo // 128) + lo % 64
-            return V("ps%d" % (2 + lo // 64 % 2), c, c + hi - lo)
         return V("ps%d" % (s[0] + lo // 128), s[1] + lo % 128, s[1] + lo % 128 + hi - lo)
 
     def sel(m, k):
         return V(m, 15 - k, 143 - k)
 
-    load("s", V("X", 0, 4096), "lit", 6000)
-    load("a", V("pci", 0, 256), "pn", 2200)
-    load("a", V("pci", 256, 512), "cn", 2400)
-    load("s", V("wi"), "wt", 2500)
-    load("s", V("ti", p1=8), "th", 2500)
-    load("s", V("NN", 0, 256), "neg", 3000)
+    load("a", V("pci", 0, 256), "pn", 0, 256, 2200)
+    load("s", V("pci", 256, 512), "cn", 0, 256, 2200)
+    load("s", V("X"), "lit", 0, 4096, 5500)
+    load("a", V("ti", p1=8), "th", 0, 1, 2500)
+    load("s", V("wi"), "wt", 0, 1, 5500)
+    load("s", V("NN", 0, 256), "neg", 0, 256, 5500)
     iota(V("pi", 0, 1), [[0, 1]], 1)
     iota(V("Ja"), [[1, 16], [0, 2]], 0)
     iota(V("Mi"), [[1, 144]], 0)
     iota(V("Mg"), [[16, 8], [0, 16]], 0)
-    Jh = V("Ja", 0, 32, 2)
+    iota(V("Ml"), [[0, 8], [1, 16]], 0)
+    Jh, Mi = V("Ja", 0, 32, 2), V("Mi", 0, 128)
     ts(V("pi", 1, 2), V("pi", 0, 1), 15, A.bitwise_and)
     ts(V("pi", 2, 3), V("pi", 0, 1), 31, A.bitwise_and)
     cp(V("col", 0, 3), V("pi", 0, 3))
     ts(col(3), col(1), 16.0, A.mult)
     ts(V("oA"), V("Ja"), col(3), A.add)
     ts(V("oB"), Jh, 32.0, A.mult, col(2), A.add)
-    for j, nm in enumerate(("pf", "CF")):
+    for j, (nm, bias) in enumerate((("pp", 0.0), ("CF", 32.0))):
         a, b = V("t1", 512 * j, 512 * j + 512), V("t2", 512 * j, 512 * j + 512)
         cp(a, IND(V("pci", 256 * j, 256 * j + 256), V("oA")))
         tr(b, a)
-        act(V(nm, 0, 256), IND(b, V("oB")), F.Copy)
+        act(V(nm, 0, 256), IND(b, V("oB")), F.Identity, bias)
     act(V("nz", 0, 1), col(1), F.Sigmoid, -128.0, 256.0, extra=1300.0)
-    ts(col(4), col(0), col(1), A.subtract, 15.0, A.add)
-    ts(col(5), col(0), 1.0, A.add)
+    iota(V("Ex"), [[1, 32], [0, 16]], 0)
+    ts(V("Ex"), V("Ex"), col(2), A.is_equal, -1.0, A.mult)
+    iota(V("BS"), [[0, 1152]], 0, 512)
+    asel(V("BS"), [[-1, 9], [-16, 8], [0, 16]], 1)
+    ts(col(15), col(0), col(1), A.subtract)
+    af(col(4), col(15), 1.0, 15.0)
+    af(col(5), col(0), 1.0, 1.0)
     ts(col(6), col(1), 15.0, A.not_equal)
     ts(col(7), col(1), 0.0, A.is_equal)
-    ts(col(8), col(7), 2304.0, A.mult, -2176.0, A.add)
+    af(col(8), col(7), 2304.0, -2176.0)
     ts(col(9), col(1), 1.0, A.is_equal, 8191.0, A.mult)
-    tt(col(10), col(9), V("nz", 0, 1), A.add)
+    af(col(10), col(9), 1.0, V("nz", 0, 1))
     ts(col(11), V("wi"), 0.0625, A.mult)
-    ts(col(12), col(1), 15.0 / 32, A.add)
-    ts(col(13), col(1), 31.0, A.mult, col(2), A.add)
-    ts(col(14), col(0), 16.0, A.mult)
+    af(col(12), col(1), 1.0, 15.0 / 32)
+    af(col(13), col(1), 31.0, col(2))
+    af(col(14), col(0), 16.0)
+    af(col(16), col(7), 8191.0, 1.0)
+    ts(col(17), col(1), 8.0, A.is_lt)
+    af(col(18), col(7), 32.0)
+    af(col(19), col(0), 1.0, 15.0)
+    af(col(23), col(7), 2.0, -1.0)
+    af(col(20), col(7), 1.0, -1.0)
     ts(V("oC"), V("Ja"), 16.0, A.mult, col(1), A.add)
     ts(V("oD"), Jh, col(13), A.add)
-    ts(V("b16"), Jh, 256.0, A.mult, col(3), A.add)
-    ts(V("bi"), Jh, 16.0, A.mult, col(12), A.add)
-    ms(V("X", 4096, 4112), -255.0)
-    ms(V("Rs"), 0.0)
-    ms(V("Rs", 0, 2048, 16), 255.0)
-    mwo, o = [], 0
-    for b, n in enumerate(BC):
-        ms(V("Mw", 16 * (o + b), 16 * (o + b) + 16), 255.0)
-        mwo += [16 * (b + 1)] * n
-        o += n
-    Mi = V("Mi", 0, 128)
+    af(V("bi"), Jh, 16.0, col(12))
+    rs = 16 * max(cfg["QC"] if cfg["Q2"] else BC)
+    ms(V("Rs", 0, rs), -256.0)
+    ms(V("Rs", 0, rs, 16), 255.0)
+    ms(V("on"), 1.0)
+    pad = []
+    for b, (lo, hi) in enumerate(chunks(BC)):
+        ms(V("Dw", 16 * (lo + b), 16 * (lo + b) + 16), 255.0)
+        ms(V("lp", 16 * (hi + b), 16 * (hi + b) + 16), 255.0)
+        pad += [16 * b] * (hi - lo)
     ts(V("SZ"), V("Mi"), col(4), A.is_equal)
-    ts(V("SH"), V("SZ"), -4096.0, A.mult)
-    ts(V("S8"), V("SZ"), 8192.0, A.mult)
-    ts(col(15), col(4), -15.0, A.add)
-    ts(col(16), col(1), 0.0, A.not_equal)
-    for j, (s, w) in enumerate((("1", col(16)), ("2", col(10)), ("W", col(11)))):
+    if len(cfg["ST"]) < 4:
+        af(V("SN"), V("SZ"), -1.0)
+        af(V("SD"), V("SZ"), 2.0)
+    ts(V("Gm"), V("Mg"), col(15), A.is_equal)
+    for j, s, w in ((0, "1", col(16)), (1, "2", col(10)), (1, "E", col(7)), (2, "W", col(11))):
         if j in cfg["PS"]:
-            ts(V("K" + s), V("Mg"), col(15), A.is_equal, w, A.mult)
+            af(V("K" + s), V("Gm"), w)
         else:
-            ts(V("S" + s), V("SZ"), w, A.mult)
+            af(V("S" + s), V("SZ"), w)
     if cfg["PS"]:
-        iota(V("Ml"), [[0, 8], [1, 16]], 0)
         ts(V("Cz"), V("Ml"), col(1), A.not_equal, -32768.0, A.mult)
-        ts(V("Cb"), Mi, 16.0, A.mult)
-        tt(V("Cb"), V("Cb"), V("Cz"), A.add)
-        ts(V("R0"), V("Ml"), 0.0, A.not_equal)
+        af(V("Dg"), Mi, 16.0)
+        tt(V("Cb"), V("Dg"), V("Cz"), A.add)
+        act(V("R0"), V("Ml"), F.Sigmoid, -128.0, 256.0)
+    if len(cfg["PS"]) < 3:
+        af(V("b16"), Jh, 256.0, col(3))
+    ts(V("Zp"), V("Mi"), col(19), A.is_equal, col(17), A.mult)
     ts(V("Ib"), Mi, col(0), A.is_equal)
-    ts(V("In"), V("Ib"), -1.0, A.mult)
-    ts(V("Ih"), V("Ib"), 0.5, A.mult)
+    af(V("In"), V("Ib"), -1.0)
+    af(V("Ih"), V("Ib"), 0.5)
     ts(V("En"), V("Mg"), col(0), A.is_equal, -1.0, A.mult)
-    ts(V("Ep"), V("En"), -256.0, A.mult)
-    ts(V("Em"), V("En"), 256.0, A.mult)
+    af(V("Ep"), V("En"), -256.0)
+    af(V("Em"), V("En"), 256.0)
     tt(V("Am"), V("Ib"), V("En"), A.add)
-    act(V("If"), V("Ib"), F.Copy)
+    af(V("If"), V("Ib"), 1.0)
+    if not cfg["UA"]:
+        ts(col(21), col(0), 1.0, A.is_equal, -37888.0, A.mult)
+        ts(col(22), col(0), 0.0, A.is_equal, -83.0 * 2 ** 17, A.mult)
+        af(col(22), col(22), 1.0, col(21))
+        af(V("Uf"), V("Ib"), 2048.0)
+        af(V("Ku"), V("on"), col(22))
     ts(V("Dt"), Mi, col(5), A.is_equal, col(6), A.mult)
-    ts(V("Dm"), V("Ib"), V("nz", 0, 1), A.mult)
-    tt(V("Dm"), V("Dt"), V("Dm"), A.subtract)
+    af(V("Dm"), V("Ib"), col(23))
+    tt(V("Dm"), V("Dm"), V("Dt"), A.add)
     tt(V("Wm"), V("Ib"), sel("SZ", 0), A.subtract)
-    tt(V("DW"), V("Dm"), sel("SZ", 1), A.subtract)
-    ts(V("Sa"), Mi, 0.0, A.mult, col(7), A.add)
+    af(V("DW"), V("Ib"), col(20))
+    tt(V("DW"), V("DW"), V("Dt"), A.add)
+    tt(V("nh", 0, 128), sel("SZ", 0), sel("SZ", 1), A.add)
+    tt(V("DW"), V("DW"), V("nh", 0, 128), A.subtract)
+    ts(V("Lm"), V("Ml"), col(1), A.is_ge, col(23), A.mult)
+    tt(V("Lm"), V("Lm"), V("Gm"), A.mult)
+    if cfg["PE"]:
+        af(V("Ln"), V("Lm"), -1.0)
+        af(V("Nf"), V("Ib"), -1.0)
+        af(V("Kp"), V("Ib"), -896.0)
+    af(V("Sa"), Mi, 0.0, col(7))
     ts(V("G8", p1=8), V("Mg", p1=8), V("col", 14, 15, p1=8), A.is_equal)
     cp(V("tf", 0, 1, p1=8), V("ti", p1=8))
-    mm([(V("ps7", 320, 321), V("G8", p1=8), V("tf", 0, 1, p1=8))])
-    ts(V("tf", 1, 2), V("ps7", 320, 321), 0.0, A.add)
-    ts(V("bz", 0, 1), V("ps7", 320, 321), -4096.0, A.mult)
-    act(V("Td"), V("If"), F.Identity, 0.0, V("bz", 0, 1))
-    ms(V("on"), 1.0)
+    mm("TH", [(V("ps7", 320, 321), V("G8", p1=8), V("tf", 0, 1, p1=8))])
+    plain, turned = len(cfg["ST"]) < 4, len(cfg["ST"]) > 0
 
-    def chunks(c, o=0):
-        out = []
-        for n in c:
-            out.append((o, o + n))
-            o += n
-        return out
+    def c2(j):
+        return V("cl2", j, j + 1)
 
-    def p_forms(lo, hi):
-        cp(V("pu", lo, hi), V("pf", lo, hi))
-        act(V("pp", lo, hi), V("pf", lo, hi), F.Identity, 1184.0)
-        act(P(UP, lo, hi), V("pf", lo, hi), F.Identity, -2555904.0, 2080.0)
+    if plain:
+        ts(V("tf", 2, 3), V("ps7", 320, 321), 65.0, A.add, col(17), A.mult)
+        af(V("tf", 1, 2), V("tf", 2, 3), 1.0, -64.5)
+        af(V("bz", 0, 1), V("tf", 1, 2), -256.0)
+    if turned:
+        cp(V("ai", 2, 3), V("ps7", 320, 321))
+        ts(V("ai", 3, 4), V("ai", 2, 3), 63, A.bitwise_and)
+        ts(c2(0), col(1), 1.0, A.is_equal, -1.0, A.mult)
+        ts(c2(1), col(1), 2.0, A.is_equal)
+        tt(c2(2), V("ai", 3, 4), V("ai", 2, 3), A.subtract)
+        af(c2(3), c2(2), col(7), c2(1))
+        ts(c2(4), V("ai", 3, 4), 0.5, A.add, c2(0), A.mult)
+        af(c2(5), c2(4), 1.0, c2(3))
+        ts(V("Tm"), V("Ml"), 8.0, A.is_ge, c2(1), A.is_equal)
+        tt(V("Tm"), V("Tm"), V("Gm"), A.mult)
+        af(V("Th"), V("Tm"), c2(5))
+        af(V("GN"), V("Gm", 0, 128, 16), -1.0)
+        af(V("GD"), V("Gm", 0, 128, 16), 2.0)
+    af(V("Zn", 0, 128), V("BS", 1024, 1152), 1.0 / 1024)
+    for h in range(2):
+        tt(V("Zo", 128 * h, 128 * h + 128), V("Zn", 0, 128), sel("Zp", 8 * h), A.subtract)
 
-    def turn_out(j, src, name):
+    def turn_out(j, src, name, bias):
         a, b = V("t1", 512 * j, 512 * j + 512), V("t2", 512 * j, 512 * j + 512)
-        act(a, IND(src, V("oC")), F.Copy)
+        act(a, IND(src, V("oC")), F.Identity, bias)
         tr(b, a)
         y = V("yo", 256 * j, 256 * j + 256)
         cp(y, IND(b, V("oD")))
         store("s", name, 0, 256, y, 2300)
 
     for lo, hi in chunks(BC):
-        p_forms(lo, hi)
+        cp(V("pu", lo, hi), V("pp", lo, hi))
+        act(P(PP, lo, hi), V("pp", lo, hi), F.Identity, -864.0)
     Xw = V("X")
     for t in range(RO):
         c0 = 256 * t
-        now[:] = ["", set()]
+        now[:] = ["", set(), t]
         for lo, hi in chunks(HC):
-            cf = V("CF", c0 + lo, c0 + hi)
-            grp[0] = "h%d" % lo
-            cp(V("cu", lo, hi), cf)
-            act(P(CT, lo, hi), cf, F.Identity, -2048.0)
-            tt(V("tq", lo, hi), P(CT, lo, hi), V("pp", lo, hi), A.mult)
-            tt(V("vi", lo, hi), P(UP, lo, hi), V("tq", lo, hi), A.add)
+            cf, u = V("CF", c0 + lo, c0 + hi), "%d" % (lo // 32)
+            ts(V("cu", lo, hi), cf, -32.0, A.add)
+            tt(V("tq", lo, hi), P(PP, lo, hi), cf, A.mult)
+            if cfg["UA"]:
+                act(P(UC, lo, hi), cf, F.Identity, -37888.0 - 83.0 * 2 ** 17, 2048.0, nm="UC" + u)
+            else:
+                mm("UC" + u, [(P(UC, lo, hi), V("Ku"), V("on", 0, hi - lo)), (P(UC, lo, hi), V("Uf"), cf)])
+            tt(V("vi", lo, hi), P(UC, lo, hi), V("tq", lo, hi), A.add)
             ts(V("hi", lo, hi), V("vi", lo, hi), 5, A.arith_shift_right, 4095, A.bitwise_and)
+            cp(V("hu", lo, hi), V("hi", lo, hi))
+        for lo in (0, 128):
+            mm("NT%d" % (lo // 32), [(P(MS, lo, lo + 128), V("NN", c0 + lo, c0 + lo + 128), V("Ib"))])
+            act(V("nT", lo, lo + 128), P(MS, lo, lo + 128), F.Copy)
         for j, (lo, hi) in enumerate(chunks(FC)):
             r0, r1 = 16 * lo, 16 * hi
-            grp[0] = "f%d" % lo
             for nm, ix, onv in (("xb", "pu", cfg["XV"]), ("yb", "cu", cfg["YV"])):
-                for a, b in chunks(cfg["GS"].get(j, [hi - lo]) if nm == "xb" or j in cfg["MXP"] else [hi - lo], lo):
-                    if j in onv:
-                        cp(V(nm, 16 * a, 16 * b), IND(Xw, V(ix, a, b)))
-                    else:
-                        act(V(nm, 16 * a, 16 * b), IND(Xw, V(ix, a, b)), F.Copy)
-            for a, b in chunks(cfg["GS"].get(j, [hi - lo]), lo):
-                y = V("yb", 16 * a, 16 * b) if j in cfg["MXP"] else IND(Xw, V("cu", a, b))
-                tt(V("mx", 16 * a, 16 * b), y, V("xb", 16 * a, 16 * b), A.max)
-            tok = "k%d" % (lo // 64 % 2)
-            for u, (s, b) in enumerate((("SH", "xb"), ("SH", "yb"), ("S8", "mx"))):
-                mm([(P(SIG, lo, hi), V("Td"), V("on", 0, hi - lo))] * (u == 0)
-                   + [(P(SIG, lo, hi), sel(s, k), V(b, r0 + k, r1, 16)) for k in range(16)], u == 0, u == 2, tok)
-            tt(V("a1", lo, hi), P(SIG, lo, hi), V("hi", lo, hi), A.max)
-            ts(V("hu", lo, hi), V("a1", lo, hi), 4096.0, A.min)
-            for a, b in chunks(cfg["LS"].get(j, [hi - lo]), lo):
-                z, a, b = IND(Xw, V("hu", a, b)), 16 * a, 16 * b
-                if j in cfg["ZA"]:
-                    act(V("zb", a, b), z, F.Copy)
-                    z = V("zb", a, b)
-                tt(V("lp", a, b), z, V("mx", a, b), A.min)
-                act(V("la", a, b), V("lp", a, b), F.Abs)
-                scan(V("Mw", mwo[lo] + a, mwo[lo] + b), V("Rs", 0, b - a), V("la", a, b))
-            for e0 in range(lo, hi, 64):
-                e1 = min(hi, e0 + 64)
-                w = 8 * (e1 - e0)
-                for par in range(2):
-                    bk = "ps%d" % par
-                    mo = mwo[lo] + 16 * e0
-                    mm([(V(bk, 0, w), V("Ib"), V("Mw", mo + par, mo + 2 * w, 2))]
-                       + [(V(bk, k, w, 8), V("In"), V("NN", c0 + e0, c0 + e1)) for k in range(8)])
-                    act(V("Bb", 1 + 16 * e0 + par, 1 + 16 * e1, 2), V(bk, 0, w), F.Sigmoid, 128.0, 256.0)
-            mm([(P(CN, lo, hi), sel("SZ", (k + 1) % 16), V("Bb", 1 + r0 + k, 1 + r1, 16)) for k in range(16)])
+                if j in onv:
+                    cp(V(nm, r0, r1), IND(Xw, V(ix, lo, hi)))
+                else:
+                    act(V(nm, r0, r1), IND(Xw, V(ix, lo, hi)), F.Copy)
+            if j in cfg["FO"]:
+                add("g", "fold", (V("mx", r0, r1), V("yb", r0, r1), V("xb", r0, r1), A.max), [V("mx", r0, r1)],
+                    [V("yb", r0, r1), V("xb", r0, r1)], ("fold", r1 - r0), sem="f%d" % j, cum=t + 1)
+            else:
+                tt(V("mx", r0, r1), V("yb", r0, r1), V("xb", r0, r1), A.max)
+            z = IND(Xw, V("hu", lo, hi))
+            if j in cfg["ZA"]:
+                act(V("zb", r0, r1), z, F.Copy)
+                z = V("zb", r0, r1)
+            elif j in cfg["ZV"]:
+                cp(V("zb", r0, r1), z)
+                z = V("zb", r0, r1)
+            tt(V("lp", pad[lo] + r0, pad[lo] + r1), z, V("mx", r0, r1), A.min)
+            if lo // 64 in cfg["ST"]:
+                if hi % 64:
+                    continue
+                lo, r0 = hi - 64, r1 - 1024
+            c = 128 * (lo // 128) + 2 * (lo % 64)
+            sg = V("ps%d" % (2 + lo // 64 % 2), c, c + 2 * (hi - lo))
+            if lo // 64 in cfg["ST"]:
+                for u, (s, b) in enumerate((("GN", "xb"), ("GN", "yb"), ("GD", "mx"))):
+                    mm("S%s%d" % (b[0], lo // 32), [(sg, V("on"), V("Th"))] * (u == 0)
+                       + [(V(sg["name"], c + k, c + 128, 16), V(b, r0 + k, r1, 8), V(s)) for k in range(8)], u == 0, u == 2)
+                act(V("nt", 2 * lo, 2 * hi), sg, F.Sigmoid, 0.0, 256.0)
+                mm("St%d" % (lo // 32), [(sg, V("nt", 2 * lo, 2 * hi), V("Ib"))])
+                act(V("nk", 2 * lo, 2 * hi), sg, F.Copy)
+            else:
+                for u, (s, b) in enumerate((("SN", "xb"), ("SN", "yb"), ("SD", "mx"))):
+                    mm("S%s%d" % (b[0], lo // 32), [(sg, sel(s, k), V(b, r0 + k, r1, 8)) for k in range(8)], u == 0, u == 2)
+                act(V("nk", 2 * lo, 2 * hi), sg, F.Sigmoid, V("bz", 0, 1), 256.0)
+            for e in range(lo, hi, 32):
+                bk, h, u = "ps%d" % (e // 32 % 2), 128 * (e // 128), "%d" % (e // 32)
+                mm("Dn" + u, [(V(bk), V("nT", h, h + 128, p0=e - h, p1=e - h + 32), V("Ex", p0=e - h, p1=e - h + 32))], True, False)
+                mm("Dk" + u, [(V(bk, s, 512, 8), V("BS", 128 * s, 128 * s + 128), V("nk", 2 * e, 2 * e + 64)) for s in range(8)], False, False)
+                mm("Dl" + u, [(V(bk), V("Ib"), V("lp", pad[e] + 16 * e, pad[e] + 16 * e + 512))], False, True)
+                scan(V("Dw", pad[e] + 16 + 16 * e, pad[e] + 16 + 16 * e + 512), V("Rs", 0, 512), V(bk))
+            fw = min(cfg["FW"], hi - lo)
+            for a in range(lo, hi, fw):
+                d, f = V("Dw", pad[a] + 16 + 16 * a, pad[a] + 16 + 16 * (a + fw)), V("Bb", 1 + 16 * a, 1 + 16 * (a + fw))
+                if a // 32 in cfg["FV"]:
+                    ts(f, d, 0.0, A.is_ge)
+                else:
+                    act(f, d, F.Sigmoid, 128.0, 256.0)
+            for a, b in chunks(cfg["QC"]):
+                if lo < b <= hi:
+                    mm("C1%d" % (a // 32), [(P(CN, a, b), sel("SZ", (k + 1) % 16), V("Bb", 1 + 16 * a + k, 1 + 16 * b, 16)) for k in range(16)])
         for b, (lo, hi) in enumerate(chunks(BC)):
-            r0, r1, h0, h1 = 16 * lo, 16 * hi, lo // 16, hi // 16
-            nh_ = h1 - h0
-            grp[0] = "b%d" % lo
-            n_, cf = V("NN", c0 + lo, c0 + hi), V("CF", c0 + lo, c0 + hi)
+            r0, r1, h0, h1, w, u = 16 * lo, 16 * hi, lo // 16, hi // 16, hi - lo, "%d" % (lo // 32)
+            n_, cf, on = V("NN", c0 + lo, c0 + hi), V("CF", c0 + lo, c0 + hi), V("on", 0, w)
 
             def L(name):
                 return V(name, lo, hi)
 
-            def picks(j, s, src, base):
+            def picks(j, srcs, base):
                 if j not in cfg["PS"]:
-                    o = P(PK, lo, lo + nh_)
-                    mm(([(o, V("Ib"), V("b16", 0, nh_))] if base else []) + [(o, sel("S" + s, il), V(src, lo + il, hi, 16)) for il in range(16)])
+                    o = P(PK, lo, lo + h1 - h0)
+                    mm("K%d%s" % (j, u), ([(o, V("Ib"), V("b16", 0, h1 - h0))] if base else [])
+                       + [(o, sel("S" + s, il), V(x["name"], x["c0"] + il, x["c1"], 16)) for s, x in srcs for il in range(16)])
                     return o
-                mm([(P(PK, lo, hi), V("Ib"), V("Cb" if base else "Cz", 0, hi - lo)), (P(PK, lo, hi), V("K" + s), L(src))])
-                add("v", "scan2", (L("pk"), V("R0", 0, hi - lo), P(PK, lo, hi)), [L("pk")], [V("R0", 0, hi - lo), P(PK, lo, hi)], ("c", hi - lo))
+                mm("K%d%s" % (j, u), [(P(PK, lo, hi), V("Ib"), V("Cb" if base else "Cz", 0, w))] + [(P(PK, lo, hi), V("K" + s), x) for s, x in srcs])
+                add("v", "scan2", (L("pk"), V("R0", 0, w), P(PK, lo, hi)), [L("pk")], [V("R0", 0, w), P(PK, lo, hi)], ("c", w), "k%d%s" % (j, u))
                 return V("pk", lo + 15, hi, 16)
 
-            tok = "n%d" % (lo // 128)
-            act(P(ZC, lo, hi), L("a1"), F.Identity, 4096.0 * 4096.0, -4096.0)
-            tt(P(ZC, lo, hi), P(ZC, lo, hi), L("pf"), A.max)
-            tt(L("Nf"), P(ZC, lo, hi), L("a1"), A.min)
-            mm([(P(DD, lo, hi), V("Dm"), L("Nf"))], tok=tok)
-            act(L("Ds"), P(DD, lo, hi), F.Copy)
+            nk = [V("nk", 2 * lo + h, 2 * hi, 2) for h in range(2)]
+            mm("OK" + u, [(P(OKP, lo, hi), V("Zo", 128 * h, 128 * h + 128), nk[h]) for h in range(2)])
+            mm("NK" + u, [(P(NKP, lo, hi), sel("Zp", 8 * h), nk[h]) for h in range(2)])
+            tt(L("w1"), P(OKP, lo, hi), L("hi"), A.mult)
+            tt(L("w2"), P(NKP, lo, hi), L("pp"), A.mult)
+            mm("DA" + u, [(P(DD, lo, hi), V("Dm"), L("w1")), (P(DD, lo, hi), V("Dm"), L("w2"))])
+            act(L("D1"), P(DD, lo, hi), F.Identity, col(18))
             act(L("nb"), P(CN, lo, hi), F.Sigmoid, -2176.0, 256.0, acc=V("acc", b, b + 1) if t < RO - 1 else None)
-            o = picks(0, "1", "nb", True)
-            cp(V("i1", h0, h1), o)
-            law = IND(V("la", r0, r1), V("i1", h0, h1))
-            act(L("lk"), law, F.Copy)
-            if b in cfg["CA"]:
-                mm([(P(PK, lo, hi), V("In"), n_), (P(PK, lo, hi), V("Ib"), L("lk"))])
-                act(V("Bb", r0, r1, 16), P(PK, lo, hi), F.Sigmoid, 128.0, 256.0)
+            o = picks(0, [("1", L("nb"))], True)
+            ts(V("i1", h0, h1), o, 16.0 * w, A.min)
+            law = IND(V("lp", r0 + 16 * b, r1 + 16 * b + 16), V("i1", h0, h1))
+            seed = V("Bb", r0, r1, 16)
+            if b in cfg["SA"]:
+                act(L("lk"), law, F.Copy)
+                mm("DK" + u, [(P(MS, lo, hi), V("In"), n_), (P(MS, lo, hi), V("Ib"), L("lk"))])
+                act(seed, P(MS, lo, hi), F.Sigmoid, 128.0, 256.0, nm="sd" + u)
+            elif b in cfg["SM"]:
+                tt(seed, law, n_, A.is_ge, nm="sd" + u)
+                act(L("lk"), law, F.Copy)
+                mm("DK" + u, [(P(MS, lo, hi), V("In"), n_), (P(MS, lo, hi), V("Ib"), L("lk"))])
+                act(L("dk"), P(MS, lo, hi), F.Copy)
             else:
-                tt(V("Bb", r0, r1, 16), law, n_, A.is_ge)
-            scan(V("B2", r0, r1), V("Rs", 0, r1 - r0), V("Bb", r0, r1))
-            mm([(P(CN, lo, hi), sel("SZ", j + 1), V("B2", r0 + j, r1, 16)) for j in range(15)])
-            mm([(P(AM, lo, hi), V("Am"), L("nb"))])
-            tt(L("ta"), P(AM, lo, hi), L("Ds"), A.mult)
-            if cfg["DA"]:
-                mm([(P(DD, lo, hi), V("DW"), L("ta"))], tok=tok)
-                tt(L("Ds"), P(DD, lo, hi), L("Ds"), A.add)
-            else:
-                mm([(P(DD, lo, hi), V("Dm"), L("Nf")), (P(DD, lo, hi), V("DW"), L("ta"))], tok=tok)
-                act(L("Ds"), P(DD, lo, hi), F.Copy)
-            mm([(P(NH, lo, hi), V("Ib"), n_), (P(NH, lo, hi), V("Ep"), L("nb"))], tok=tok)
-            act(L("nh"), P(NH, lo, hi), F.Identity, -256.0)
-            mm([(P(N2, lo, hi), V("If"), L("Nf")), (P(N2, lo, hi), V("Wm"), L("ta"))], True, False, tok)
+                tt(L("dk"), law, n_, A.subtract)
+                ts(seed, L("dk"), 0.0, A.is_ge, nm="sd" + u)
+            for a, e in chunks(cfg["QC"]) if cfg.get("Q2") else [(lo, hi)]:
+                if lo <= a < hi:
+                    scan(V("B2", 16 * a, 16 * e), V("Rs", 0, 16 * (e - a)), V("Bb", 16 * a, 16 * e))
+                    mm("C2%d" % (a // 32), [(P(CN, a, e), sel("SZ", j + 1), V("B2", 16 * a + j, 16 * e, 16)) for j in range(15)])
+            mm("A1" + u, [(P(AM, lo, hi), V("Am"), L("nb"))])
+            tt(L("ta"), P(AM, lo, hi), L("D1"), A.mult)
+            mm("DB" + u, [(P(DD, lo, hi), V("If"), L("D1")), (P(DD, lo, hi), V("DW"), L("ta"))])
+            act(L("D2"), P(DD, lo, hi), F.Copy)
+            if b not in cfg["MA"]:
+                mm("NH" + u, [(P(NH, lo, hi), V("Ib"), n_), (P(NH, lo, hi), V("Ep"), L("nb"))])
+                act(L("nh"), P(NH, lo, hi), F.Identity, -256.0)
+            if cfg["PE"]:
+                mm("EE" + u, [(P(EE, lo, hi), V("If"), cf), (P(EE, lo, hi), V("Ln"), L("D2"))])
+            mm("Na" + u, [(P(N2, lo, hi), V("Lm"), L("D2"))], True, False)
+            if cfg["PE"]:
+                mm("Pa" + u, [(P(PP, lo, hi), V("Kp"), on), (P(PP, lo, hi), V("If"), cf)], True, False)
             act(L("kp"), P(CN, lo, hi), F.Sigmoid, col(8), 256.0)
-            mm([(P(AM, lo, hi), V("En"), L("nb")), (P(AM, lo, hi), V("Ib"), L("kp"))])
-            tt(L("tb"), P(AM, lo, hi), L("Ds"), A.mult)
-            mm([(P(N2, lo, hi), V("Wm"), L("tb"))], False, True, tok)
-            o = picks(1, "2", "kp", True)
+            mm("A2" + u, [(P(AM, lo, hi), V("En"), L("nb")), (P(AM, lo, hi), V("Ib"), L("kp"))])
+            tt(L("tb"), P(AM, lo, hi), L("D2"), A.mult)
+            mm("Nb" + u, [(P(N2, lo, hi), V("Wm"), L("tb"))], False, True)
+            sc = V("SC", c0 + lo, c0 + hi)
+            act(sc, P(N2, lo, hi), F.Copy)
+            send(V("CF", c0 + 256 + lo, c0 + 256 + hi), sc, t)
+            if cfg["PE"]:
+                tt(L("tc"), P(EE, lo, hi), L("kp"), A.mult)
+                mm("Pb" + u, [(P(PP, lo, hi), V("Nf"), L("tc"))], False, False)
+                mm("Pc" + u, [(P(PP, lo, hi), V("Wm"), L("tb"))], False, True)
+                if t < RO - 1:
+                    ts(L("pu"), P(PP, lo, hi), 864.0, A.add)
+                act(L("pp"), P(PP, lo, hi), F.Identity, 864.0)
+            else:
+                tt(P(EE, lo, hi), P(N2, lo, hi), cf, A.subtract, nm="u1" + u)
+                tt(P(EE, lo, hi), P(EE, lo, hi), L("kp"), A.mult, nm="u2" + u)
+                tt(L("tc"), P(EE, lo, hi), cf, A.add)
+                if t < RO - 1:
+                    ts(L("pu"), L("tc"), -32.0, A.add)
+                    act(P(PP, lo, hi), L("tc"), F.Identity, -896.0, nm="PP" + u)
+                act(L("pp"), L("tc"), F.Identity, -32.0)
+            o = picks(1, [("E", L("nb")), ("2", L("kp"))], True)
             ts(V("i2", h0, h1), o, 16.0 - 8192.0, A.add, 0.0, A.max)
-            m0 = 16 * (lo + b)
-            tt(L("Mm"), IND(V("Mw", m0, m0 + 16 + r1 - r0), V("i2", h0, h1)), L("lk"), A.min)
-            o = picks(2, "W", "Mm", False)
-            tt(V("qq", h0, h1), o, V("bi", 0, nh_), A.subtract)
+            dw = IND(V("Dw", r0 + 16 * b, r1 + 16 * b + 16), V("i2", h0, h1))
+            if b in cfg["SA"]:
+                act(L("dp"), dw, F.Copy)
+                tt(L("DM"), P(MS, lo, hi), L("dp"), A.min)
+            else:
+                tt(L("DM"), dw, L("dk"), A.min)
+            o = picks(2, [("W", n_), ("W", L("DM"))], False)
+            tt(V("qq", h0, h1), o, V("bi", 0, h1 - h0), A.subtract)
             tt(V("ff", h0, h1), o, V("qq", h0, h1), A.subtract)
             ts(V("i3", h0, h1), V("ff", h0, h1), 16.0, A.mult)
-            mm([(P(VL, lo, hi), V("Ih"), n_), (P(VL, lo, hi), V("Ih"), L("Mm"))], tok=tok)
+            mm("VL" + u, [(P(VL, lo, hi), V("Ib"), n_), (P(VL, lo, hi), V("Ih"), L("DM"))])
             if b in cfg["VA"]:
-                act(L("vf"), P(VL, lo, hi), F.Identity, 12582912.0, 1.0 - 2.0 ** -10)
-                act(L("vb"), L("vf"), F.Identity, -12582912.0)
+                af(L("vf"), P(VL, lo, hi), 1.0 - 2.0 ** -10, 12582912.0)
+                af(L("vb"), L("vf"), 1.0, -12582912.0)
                 cp(IND(V("X", r0, r1), V("i3", h0, h1)), L("vb"))
             else:
                 ts(L("vl"), P(VL, lo, hi), -0.25, A.add)
                 cp(IND(V("X", r0, r1), V("i3", h0, h1)), L("vl"))
             sm = V("SM", c0 + lo, c0 + hi)
-            if b in cfg["SA"]:
-                mm([(P(PA, lo, hi), V("Em"), L("nb")), (P(PA, lo, hi), V("In"), L("nh")), (P(PA, lo, hi), V("Ib"), L("Mm"))], tok=tok)
-                act(L("vf"), P(PA, lo, hi), F.Relu)
-                mm([(P(PA, lo, hi), V("Ib"), L("nh")), (P(PA, lo, hi), V("If"), L("vf"))], tok=tok)
-                act(sm, P(PA, lo, hi), F.Copy)
+            if b in cfg["MA"]:
+                for nm, sg in (("r1", "Ib"), ("r2", "In")):
+                    mm(nm.upper() + u, [(P(AM, lo, hi), V("Em"), L("nb")), (P(AM, lo, hi), V(sg), L("DM"))])
+                    act(L(nm), P(AM, lo, hi), F.Relu)
+                mm("PA" + u, [(P(MS, lo, hi), V("Ib"), n_), (P(MS, lo, hi), V("Ib"), L("r1")), (P(MS, lo, hi), V("In"), L("r2"))])
+                act(sm, P(MS, lo, hi), F.Copy)
             else:
-                mm([(P(PA, lo, hi), V("Em"), L("nb")), (P(PA, lo, hi), V("Ib"), L("Mm"))], tok=tok)
-                tt(sm, P(PA, lo, hi), L("nh"), A.max)
+                mm("PA" + u, [(P(MS, lo, hi), V("Em"), L("nb")), (P(MS, lo, hi), V("Ib"), n_), (P(MS, lo, hi), V("Ib"), L("DM"))])
+                tt(sm, P(MS, lo, hi), L("nh"), A.max)
             send(V("NN", c0 + 256 + lo, c0 + 256 + hi), sm, t)
-            sc = V("SC", c0 + lo, c0 + hi)
-            act(sc, P(N2, lo, hi), F.Copy)
-            send(V("CF", c0 + 256 + lo, c0 + 256 + hi), sc, t)
-            tt(P(QR, lo, hi), P(N2, lo, hi), cf, A.subtract)
-            tt(P(QR, lo, hi), P(QR, lo, hi), L("kp"), A.mult)
-            tt(L("pf"), P(QR, lo, hi), cf, A.add)
-            if t < RO - 1:
-                p_forms(lo, hi)
-            else:
+            if t == RO - 1:
                 store("s", "yx", r0, r1, V("X", r0, r1), 1800 + 4200 * (hi - lo) // NL)
         if t < RO - 1:
             o = V("ps7", 128, 129)
-            mm([(o, V("Sa"), V("acc", b, b + 1)) for b in range(len(BC))])
+            mm("AS", [(o, V("Sa"), V("acc", b, b + 1)) for b in range(len(BC))])
             cp(V("ai", 0, 1), o)
             ts(V("ai", 1, 2), V("ai", 0, 1), 63, A.bitwise_and)
-            ts(V("bz", 0, 1), V("ai", 1, 2), V("tf", 1, 2), A.add, -4096.0, A.mult)
-            act(V("Td"), V("If"), F.Identity, 0.0, V("bz", 0, 1))
-    now[:] = ["e", set()]
-    turn_out(0, V("pf"), "yp")
-    turn_out(1, V("CF", 256 * RO, 256 * RO + 256), "yc")
+            if plain:
+                ts(V("bz", 0, 1), V("ai", 1, 2), V("tf", 1, 2), A.add, -256.0, A.mult)
+            if turned:
+                ts(V("bz", 1, 2), V("ai", 1, 2), c2(0), A.mult, c2(5), A.add)
+                af(V("Th"), V("Tm"), V("bz", 1, 2))
+    now[:] = ["e", set(), RO]
+    turn_out(0, V("pp"), "yp", 0.0)
+    turn_out(1, V("CF", 256 * RO, 256 * RO + 256), "yc", -32.0)
     store("a", "yn", 0, 256, V("NN", 256 * RO, 256 * RO + 256), 2200)
 
-    seen = {}
+    seen, starts, closed = {}, {}, {}
     for i, o in enumerate(ops):
         dep = set()
         for kind, lst in (("r", o["r"]), ("w", o["w"])):
@@ -438,9 +544,19 @@ def build(cfg):
                     if c < b and a < d and (kind == "w" or k2 == "w"):
                         dep.add(j)
         for nm, a, b in o["w"]:
-            seen[nm] = [e for e in seen.get(nm, ()) if not (a <= e[2] and e[3] <= b and o["kind"] != "x")] + [(i, "w", a, b)]
+            seen[nm] = [e for e in seen.get(nm, ()) if not (a <= e[2] and e[3] <= b)] + [(i, "w", a, b)]
         for nm, a, b in o["r"]:
             seen.setdefault(nm, []).append((i, "r", a, b))
+        if o["kind"] == "mm":
+            bk = o["w"][0][0]
+            if o["start"]:
+                dep.update(closed.get(bk, ()))
+                if not o["stop"]:
+                    dep.update(starts.pop(bk, ()))
+                else:
+                    starts.setdefault(bk, []).append(i)
+            elif o["stop"]:
+                closed[bk] = [i]
         dep.discard(i)
         o["dep"] = dep
         o["banks"] = sorted(set(nm for nm, a, b in o["r"] + o["w"] if nm.startswith("ps")))
@@ -453,101 +569,46 @@ def times(o, C):
         return 100.0, float(n)
     if k == "rem":
         return 400.0, C["rem"]
+    if k == "fold":
+        return 400.0, 2 * C["rem"] + n * C["fb"]
     if k == "pe":
         d = n * C["pe"] + C["fp"] * o["cnt"]
         return d, d + 60.0
     f = C["fa"] if o["eng"] == "a" else C["fv"]
-    per = {"G": C["G"], "S": C["S"], "tt2": C["tt2"], "c": 1.0}[k]
-    d = f + max(n * per, 30.0) * C["cyc"] + o.get("extra", 0.0)
+    per = {"G": C["G"], "Gt": C["G"] + C["Gop"], "S": C["S"], "tt2": C["tt2"], "c": 1.0}[k]
+    d = f + max(n * per, C["mn"]) * C["cyc"] + o.get("extra", 0.0)
     return d, d
 
 
-def run(ops, C, order=None, prio=PRIO, passes=6):
-    n = len(ops)
-    tm = [times(o, C) for o in ops]
-    free, bank, fin, out = {}, {}, [0.0] * n, []
-
-    def start(i):
-        o = ops[i]
-        s = free.get(o["eng"], 0.0)
-        for j in o["dep"]:
-            s = max(s, fin[j] + C["hop"])
-        for b in o["banks"]:
-            for e, f in bank.get(b, {}).items():
-                if e != o["eng"]:
-                    s = max(s, f + C["hop"])
-        return s
-
-    def place(i, s):
-        o = ops[i]
-        free[o["eng"]] = s + tm[i][0]
-        fin[i] = s + tm[i][1]
-        for b in o["banks"]:
-            bank.setdefault(b, {})[o["eng"]] = fin[i]
-        out.append(i)
-
-    if order is not None:
-        for i in order:
-            place(i, start(i))
-        return out, max(fin), fin
+def in_order(ops):
+    names = ORDER.split()
+    place = {x.strip("<>"): j + len(names) * (x.count("<") - x.count(">")) for j, x in enumerate(names)}
+    rank = [len(names) * min(max(o["rnd"], 0), RO - 1) + place.get(o["key"], 0) for o in ops]
+    left = [len(o["dep"]) for o in ops]
     succ = [[] for _ in ops]
     for i, o in enumerate(ops):
         for j in o["dep"]:
             succ[j].append(i)
-    pred = [sorted(o["dep"]) for o in ops]
-    hop = C["hop"]
-
-    def sgs(pri, pre, suc, back):
-        busy, st, en = {}, [0.0] * n, [0.0] * n
-        left = [len(x) for x in pre]
-        ready = [i for i in range(n) if left[i] == 0]
-        while ready:
-            i = max(ready, key=lambda j: pri[j])
-            ready.remove(i)
-            o = ops[i]
-            d0, d1 = tm[i]
-            lead = d1 - d0 if back else 0.0
-            s = max([en[j] + hop for j in pre[i]] + [0.0])
-            res = [(o["eng"], lead, d0, 0.0)] + [(b, 0.0, d1, hop) for b in o["banks"]]
-            moved = True
-            while moved:
-                moved = False
-                for r, a, d, gap in res:
-                    lst = busy.setdefault(r, [])
-                    u = len(lst)
-                    while u and lst[u - 1][1] + gap > s + a:
-                        u -= 1
-                    for x, y, e in lst[u:]:
-                        if (gap == 0.0 or e != o["eng"]) and x - gap < s + a + d and s + a < y + gap:
-                            s = y + gap - a
-                            moved = True
-            for r, a, d, gap in res:
-                lst = busy[r]
-                u = len(lst)
-                while u and lst[u - 1][1] > s + a + d:
-                    u -= 1
-                lst.insert(u, (s + a, s + a + d, o["eng"]))
-            st[i], en[i] = s, s + d1
-            for j in suc[i]:
-                left[j] -= 1
-                if left[j] == 0:
-                    ready.append(j)
-        return st, en
-
-    pr = [0.0] * n
-    for i in range(n - 1, -1, -1):
-        pr[i] = tm[i][1] + hop + max([pr[j] for j in succ[i]] + [0.0])
-    pr = [pr[i] + prio.get(ops[i]["key"], 0.0) for i in range(n)]
-    best = None
-    for _ in range(passes):
-        st, en = sgs(pr, pred, succ, False)
-        order = sorted(range(n), key=lambda i: (st[i], i))
-        res = run(ops, C, order)
-        if best is None or res[1] < best[1]:
-            best = res
-        if passes > 1:
-            pr = sgs(res[2], succ, pred, True)[1]
-    return best
+    at, first = -2.0 * len(names), {}
+    for x in SETUP.split():
+        if x[0] == "@":
+            at = place[x[1:]] - 0.5
+        else:
+            at += 0.001
+            first["s" + x] = at
+    for i, o in enumerate(ops):
+        if o["rnd"] < 0:
+            rank[i] = first.get(o["key"], -3.0 * len(names))
+    ready, out = [i for i in range(len(ops)) if not left[i]], []
+    while ready:
+        i = min(ready, key=lambda j: (rank[j], j))
+        ready.remove(i)
+        out.append(i)
+        for j in succ[i]:
+            left[j] -= 1
+            if not left[j]:
+                ready.append(j)
+    return out
 
 
 def waits(ops, order):
@@ -573,12 +634,12 @@ def waits(ops, order):
                     kn[s2] = c2
         out[i] = ws
         if "sem" in o:
-            mark[i] = (o["sem"], 16, len(mark))
+            mark[i] = (o["sem"], o.get("cum", 16), len(mark))
         else:
             s = csem[o["eng"]]
             cnt[s] = cnt.get(s, 0) + 1
             mark[i] = (s, cnt[s], len(mark))
-        clock[i] = dict(kn)
+        clock[i] = {} if "cum" in o else dict(kn)
         for b in o["banks"]:
             lastb.setdefault(b, {})[o["eng"]] = i
     return out, mark, cnt
@@ -590,19 +651,26 @@ PLAN = {}
 def plan():
     if not PLAN:
         ops = build(CFG)
-        keys = list(dict.fromkeys(o["key"] for o in ops))
-        prio = {k: 100.0 * (int(PR[2 * i:2 * i + 2], 36) - 648) for i, k in enumerate(keys) if 2 * i < len(PR)}
-        order = run(ops, COST, prio=prio, passes=1)[0]
+        order = in_order(ops)
         PLAN["p"] = (ops, order) + waits(ops, order)
     return PLAN["p"]
+
+
+def helpers(T, topo):
+    out = {}
+    for c in T.cores:
+        free = [x for x in topo.cores_of(c) if T.rank_of(x) is None and x not in out.values()]
+        out[c] = min(free, key=lambda x: (topo.die(x) != topo.die(c), x))
+    return out
 
 
 def emit(o, ws, mark, g, core, T, topo):
     q = {"v": g.vector, "a": g.scalar, "p": g.tensor, "g": g, "s": g.sync}[o["eng"]]
     rank = T.rank_of(core)
     n = len(T.cores)
+    lanes = len(topo.engines(T.cores[rank - 1], core))
     for s, c in ws:
-        q.wait_ge(T.sem[s], c)
+        q.wait_ge(T.sem[s], c * lanes if s[0] in "rf" else c)
     k, a = o["kind"], [ap(T, x) for x in o["args"]]
     if k == "cp":
         ins = q.tensor_copy(a[0], a[1])
@@ -619,7 +687,7 @@ def emit(o, ws, mark, g, core, T, topo):
     elif k == "tr":
         ins = q.transpose(a[0], a[1])
     elif k == "act":
-        if a[2] in (F.Copy, F.Abs, F.Relu):
+        if a[2] in (F.Copy, F.Relu):
             ins = q.activation(a[0], a[1], a[2])
         elif a[5] is None:
             ins = q.activation(a[0], a[1], a[2], bias=a[3], scale=a[4])
@@ -630,13 +698,21 @@ def emit(o, ws, mark, g, core, T, topo):
             ins = q.matmul(ap(T, m[0]), ap(T, m[1]), ap(T, m[2]), j == 0 and o["start"], j == len(a) - 1 and o["stop"])
     elif k == "iota":
         if SCRATCH[o["args"][0]["name"]][2] == I32:
-            ins = q.iota(a[0], a[1], 0, a[2])
+            ins = q.iota(a[0], a[1], a[3], a[2])
         else:
-            ins = q.iota(a[0], a[1], 0, a[2], allow_small_or_imprecise_dtypes=True)
+            ins = q.iota(a[0], a[1], a[3], a[2], allow_small_or_imprecise_dtypes=True)
+    elif k == "asel":
+        ins = q.affine_select(a[0], a[0], a[1], A.is_equal, 0.0, 0, a[2])
     elif k == "load":
         ins = q.dma_start(a[0], T[a[1]][:])
     elif k == "store":
         ins = q.dma_start(T[a[0]][:, a[1]:a[2]], a[3])
+    elif k == "fold":
+        dst = helpers(T, topo)[core]
+        rid, pid, _ = topo.addr(dst)
+        q.remote_dma_fused([RemoteDMATransfer(dst_ids=[DstId(rid=rid, pnc=pid)], dma_engine_mask=topo.mask(core, dst), remote_sem=T.sem[o["sem"]],
+                                              srcs=[a[1], a[2]], dsts=[a[0]], alu_op=2)], local_sem=T.sem["loc"])
+        return len(topo.engines(core, dst))
     else:
         dst = T.cores[(rank + 1 + a[2] % 3) % n]
         rid, pid, _ = topo.addr(dst)
@@ -647,10 +723,22 @@ def emit(o, ws, mark, g, core, T, topo):
 
 
 def rank_program(g, core, T, topo):
-    if T.rank_of(core) is None:
-        return
     ops, order, ws, mark, cnt = plan()
     loc = 0
+    if T.rank_of(core) is None:
+        for c, h in helpers(T, topo).items():
+            if h == core:
+                rid, pid, _ = topo.addr(c)
+                for i in order:
+                    o = ops[i]
+                    if o["kind"] == "fold":
+                        g.wait_ge(T.sem[o["sem"]], o["cum"] * len(topo.engines(c, h)))
+                        x = ap(T, o["args"][0])
+                        g.remote_dma(x, x, T.sem[o["sem"]], T.sem["loc"], pid, rid, topo.mask(h, c))
+                        loc += len(topo.engines(h, c))
+        if loc:
+            g.wait_ge(T.sem["loc"], loc)
+        return
     for i in order:
         loc += emit(ops[i], ws[i], mark[i], g, core, T, topo)
     for s, c in cnt.items():

import numpy as np
from concourse.bass import DstId, RemoteDMATransfer
from concourse.mybir import AluOpType as A, ActivationFunctionType as F

RO, NL = 5, 256
CFG = dict(FC=[32, 32, 64, 64, 32, 32], QC=[64, 64, 64, 64], BC=[128, 128], HC=[128, 128], FW=32, XV=(), YV=(), ZA=(3,), ZV=(), FO=(),
           FV=(), PS=(0, 1, 2), SA=(), SM=(0, 1), UA=True, PE=False, Q2=1, ST=(0, 1, 2, 3), VA=(), MA=())
ORDER = "sBS768 swi0> pu0< scol24 scol3> soD0 X4< X0< nT0 sWm0 stf0 cu0 u14< C16 scol7 tq0 ta4 K04 scol11 Dn1> Sx1 NN0< sAm0 yx4< Dw0 SM4< sCb0 K00 sSZ0 k10 sRs0+ son0 k24 scol17 tq4 sNN0> ai0< NH0 C26 yb0> Sy0 spu128 A14 hu0> bz0 sd4 spp0> eyn0<< snz0> scol6 xb1 mx0 Sx2 sEn0 cu4 Dn5 xb2 pu4 stf1 mx1 C14 Dn4 sDw0 vi4 lp0 soA0> yb2 lp2 sIb0> sBS384 scol4> eyo0<< nk0 PP4< sBS0 nk1 nk2 xb4 yb4 Sm2 spi1> Bb6 sps50> vl4 u24 eyo256< DA4 Sy4 Dw5 Sx4 Dn2 Dw1 UC4 sG80> yb6 Sx0> sZn0 SC4 Dl2 xb6 mx4 Dn0> w14 B22 hi4 sDw2064 K14 xb7 slp2048 SM0 NN4< Dk3 DK0 yb7 tb0 Sx6 Dw4 vl0 et2512<< Dl3 Sy6 Dw2 Sm4 hu4 tb4 mx6 scol5> OK0 Sx7 hi0> OK4 nk4 sDW0+ spci0> B20 Dw3 Sy7 Dk5 NK0 sEp0 Bb1 Bb0 et20<< sX0> lp1> Dk4 lp6 mx7 C12 eyp0< et1512< Sm7 scol12> sK10 sti0> scol19> lp4 scol15>> lp7 Dl4 Bb2 Dk0> sDt0 sCF0> sDW0++ nk6 ai1 et10< C10 Dl5 nk7 sMg0>> Bb3 Sm1> DK4 spci256> sK20 Dn6 Dn3> sps40> vi0>> sEx0> soB0> Dn7 Dk6 sbi0> scol23 scol20 Dk7 ta0 Sy2> Dl6 NT0> scol16 sDm0> Dl7 nb0 PP0 sZp0> sR00 sEm0 NK4 A10 w20 w10 spi0> Bb4 sBS128> CF0 sIn0 st10> nh4> Sm0> lk0 pp4< DA0 Bb5 scol8 k04 Dw6 scol9 snh0> sSN0> Dw7 slp4112> sBS640> lk4 A24 scol10 k00 w24 C24 sd0 Sm6> D10 i10> i20 scol18 CF4> A20 scol13> sLm0+ nb4 DB0 sTH> C22 sbz0> sIf0 sDg0> yb1> sBS896> K10 sKE0 sKW0 st1512> Dl0>> st20>> C20 soC0> sMi0> B24 Dk1> i14 sIh0 B26 pp0 spi2> D14 st2512> dk0 kp0 Sy1> sMl0> tc4 eyc0< u10 D20 dk4 Bb7> DM0 k14 DB4 kp4 sSa0 sDm0+> yx0 D24 nh0 i24 Na0> Dl1> sLm0> Nb0 spu0> scol0> K20 sDW0> sEx0+> NH4 Na4 DM4 u20 PA0 SC0 sRs0> k20 Nb4 VL4 sJa0>> sCz0> Dk2> qq0 sSD0> sBS512> K24 VL0 qq4 zb4> NT4> AS UC0> mx2> tc0 sGm0> ff4 ff0 i34 scol14> sBS256>> PA4 i30 xb0> nT4>"
CFG.update(ZA=(3,), YV=(0,), FV=(7,))
ORDER = "xb1 xb0 ai0< u14< tq0 ai1< cu0 bz1< u24< yb0 UC0 vi0 yb1 Th0< tc4< mx0 hi0 pu4< mx1 hu0 lp0 lp1 xb2 yb2 mx2 cu4 lp2 NT0 Sx0 Sy0 nT0 Sx2 Sm0 NT4 nt0 Dn1 St0 Dn0 Sy2 Sm2 xb4 nk0 Dk0 Dk1 yb6 nt2 yb4 Dl0 Dw0 St2 nk2 Dl1 Dw1 Sx4 Dn2 Sy4 mx4 Dn3 Dk2 Sm4 UC4 PP4< tq4 xb6 mx6 xb7 vi4 hi4 hu4 Dk3 Dl2 Dw2 Sx6 Dl3 Dw3 nT4 yb7 nt4 St4 OK0 Dn4 mx7 Sy6 w10 zb4 lp4 lp6 nk4 Dn5 Sm6 Dk5 NK0 Dk4 Dl5 Dl4 Dw4 Dw5 Bb3 Bb2 C12 Bb0 Bb1 C10 nt6 St6 pp4< et10< et20< eyo0< eyn0< eyp0< et1512< et2512< eyo256< eyc0< nb0 nk6 Bb4 Dn6 Dn7 K00 Dk6 NH0 nh0 Dk7 Dl6 lp7 Dl7 k00 i10 w20 DA0 lk0 Bb5 sd0 Dw6 Dw7 Bb7 D10 A10 ta0 C14 OK4 NK4 Bb6 C16 nb4 B20 C20 w24 B22 K04 w14 k04 i14 sd4 lk4 B24 B26 C22 DK0 kp0 DA4 D14 DK4 K10 A20 A14 dk0 C24 k10 i20 ta4 DB0 D20 C26 dk4 kp4 DM0 K20 k20 tb0 Na0 VL0 qq0 vl0 ff0 K14 k14 i30 i24 DM4 NH4 Nb0 SC0 CF0 u10 DB4 D24 A24 nh4 PA4 K24 X0 yx0 u20 SM4 k24 NN4 tb4 qq4 VL4 PA0 SM0 NN0 Na4 Nb4 SC4 CF4 AS ff4 tc0 pp0 PP0 vl4 i34 pu0 X4 yx4"
SETUP = "pci0 X0 Rs0 pi0 pi2 pi1 Ml0 lp2048 lp4112 ti0 col0 col6 col14 Cz0 cl21 col9 nz0 col15 col7 col23 col16 col20 col8 col12 col3 col5 col10 cl20 col19 Mg0 G80 Gm0 En0 Em0 Ep0 K10 col4 col18 Ja0 oA0 oC0 t10 oB0 t20 pp0 ps50 ps40 R00 col17 GD0 pci256 t1512 tf0 GN0 Rs0+ t2512 CF0 pu128 pu0 TH ai2 Dw0 NN0 on0 Tm0 ai3 @tq0 Ex0 Ex0+ @cu0 Tm0+ @yb0 Lm0 cl22 cl23 @vi0 BS0 BS0+ Zn0 @mx0 cl24 cl25 Th0 Mi0 Ib0 Dt0 Zp0 SZ0 Am0 Wm0 DW0 In0 Ih0 Zo128 Dm0 Zo0 @lp0 DW0+ @nt2 Dm0+ @Dl0 wi0 col11 @mx7 nh0 @C10 Dg0 Cb0 @St6 K20 @nb0 KW0 @Dn6 If0 @lk0 Sa0 @Bb7 bi0 @nh0 DW0++ @sd4 KE0 @lk4 col13 oD0 @DM0 Dw2064 @K20 Lm0+"
BF, F32, I32, U16 = "bfloat16", "float32", "int32", "uint16"


def sb(n, d):
    return ("sbuf", [128, n], d)


SCRATCH = {
    "X": sb(4096, BF), "xb": sb(4096, BF), "yb": sb(4096, BF), "zb": sb(4096, BF), "mx": sb(4096, BF), "lp": sb(4096 + 128, BF),
    "Dw": sb(4096 + 128, BF), "Bb": sb(4112, BF), "B2": sb(4096, BF), "Rs": sb(4096, BF), "Ex": sb(512, BF), "BS": sb(1152, BF),
    "pci": sb(512, I32), "t1": sb(1024, F32), "t2": sb(1024, F32), "yo": sb(512, F32),
    "CF": sb(256 * (RO + 1), F32), "NN": sb(256 * (RO + 1), BF), "SC": sb(256 * RO, F32), "SM": sb(256 * RO, BF),
    "pp": sb(256, F32), "pu": sb(256, U16), "cu": sb(256, U16), "hu": sb(256, U16),
    "tq": sb(256, F32), "vi": sb(256, I32), "hi": sb(256, I32), "w1": sb(256, F32), "w2": sb(256, F32), "nk": sb(512, BF), "nt": sb(512, BF), "vf": sb(256, F32), "vb": sb(256, BF), "r1": sb(256, BF), "r2": sb(256, BF),
    "GN": sb(8, BF), "GD": sb(8, BF), "Th": sb(128, BF), "Tm": sb(128, BF), "cl2": sb(16, F32), "Zo": sb(256, BF),
    "D1": sb(256, F32), "D2": sb(256, F32), "ta": sb(256, F32), "tb": sb(256, F32), "tc": sb(256, F32), "nb": sb(256, BF), "kp": sb(256, BF),
    "lk": sb(256, BF), "dk": sb(256, BF), "dp": sb(256, BF), "DM": sb(256, BF), "nh": sb(256, BF), "nT": sb(256, BF), "vl": sb(256, I32),
    "i1": sb(16, U16), "i2": sb(16, U16), "i3": sb(16, U16), "qq": sb(16, I32), "ff": sb(16, F32),
    "acc": sb(8, F32), "ai": sb(4, I32), "bz": sb(4, F32),
    "wi": sb(1, I32), "ti": sb(1, I32), "tf": sb(4, F32), "pi": sb(4, I32), "col": sb(32, F32), "nz": sb(2, BF),
    "Mi": sb(144, F32), "Mg": sb(128, F32), "Ml": sb(128, F32), "Ja": sb(32, F32),
    "oA": sb(32, U16), "oB": sb(16, U16), "oC": sb(32, U16), "oD": sb(16, U16), "b16": sb(16, BF), "bi": sb(16, F32),
    "Ib": sb(128, BF), "In": sb(128, BF), "Ih": sb(128, BF), "Am": sb(128, BF), "En": sb(128, BF), "Ep": sb(128, BF), "Em": sb(128, BF),
    "SZ": sb(144, BF), "SN": sb(144, BF), "SD": sb(144, BF), "SW": sb(144, BF), "S1": sb(144, BF), "S2": sb(144, BF), "SE": sb(144, BF),
    "K1": sb(128, BF), "K2": sb(128, BF), "KW": sb(128, BF), "KE": sb(128, BF), "Cz": sb(128, BF), "Cb": sb(128, BF), "R0": sb(128, F32),
    "Gm": sb(128, BF), "Zp": sb(144, BF), "Zn": sb(144, BF), "on": sb(128, BF), "Kp": sb(128, BF), "Ku": sb(128, BF), "pk": sb(256, F32),
    "If": sb(128, F32), "Nf": sb(128, F32), "Uf": sb(128, F32), "Dm": sb(128, F32), "Lm": sb(128, F32), "Ln": sb(128, F32), "Wm": sb(128, F32),
    "DW": sb(128, F32), "Dt": sb(128, F32), "Dg": sb(128, F32), "Sa": sb(128, F32), "G8": sb(128, F32),
}
for _b in range(8):
    SCRATCH["ps%d" % _b] = ("psum", [128, 512], F32)
SEMAPHORES = ["cv", "ca", "cp", "cg", "loc"] + ["d%d" % i for i in range(24)] + ["r%d" % i for i in range(8 * RO)] + ["f%d" % i for i in range(8)]

COST = dict(G=1.56, Gop=0.5, S=3.8, tt2=1.0, cyc=0.83, pe=0.42, fv=40.0, fa=50.0, mn=50.0, fp=10.0, hop=120.0, rem=2000.0, fb=2.0)


def V(name, c0=0, c1=None, st=1, p0=0, p1=128, off=None):
    if c1 is None:
        c1 = SCRATCH[name][1][1]
    return dict(name=name, c0=c0, c1=c1, st=st, p0=p0, p1=p1, off=off)


def IND(win, off):
    w = dict(win)
    w["off"] = off
    return w


def width(v):
    if v["off"] is not None:
        return 16 * width(v["off"])
    return (v["c1"] - v["c0"] + v["st"] - 1) // v["st"]


def ap(T, v):
    if not isinstance(v, dict):
        return v
    t = T[v["name"]]
    r = t[v["p0"]:v["p1"], v["c0"]:v["c1"]] if v["st"] == 1 else t[v["p0"]:v["p1"], v["c0"]:v["c1"]:v["st"]]
    if v["off"] is not None:
        return r.indirect(ap(T, v["off"]))
    return r


def isps(v):
    return v["name"].startswith("ps")


def two(v):
    return SCRATCH[v["name"]][2] in (BF, U16)


def spans(vs):
    out = []
    for v in vs:
        if isinstance(v, dict):
            out.append((v["name"], v["c0"], v["c1"]))
            if v["off"] is not None:
                out.append((v["off"]["name"], v["off"]["c0"], v["off"]["c1"]))
    return out


def chunks(c, o=0):
    out = []
    for n in c:
        out.append((o, o + n))
        o += n
    return out


def build(cfg):
    ops = []
    FC, BC, HC = cfg["FC"], cfg["BC"], cfg["HC"]
    now = ["s", set(), -1]

    def add(eng, kind, args, outs, ins, n, nm=None, **kw):
        w = [(v["name"], v["c0"], v["c1"]) for v in outs]
        r = spans(ins) + [(v["off"]["name"], v["off"]["c0"], v["off"]["c1"]) for v in outs if v["off"] is not None]
        if nm is None:
            nm, c = (w or r)[0][:2]
            wide = SCRATCH[nm][1][1]
            if now[0] == "":
                c = c // 512 if wide >= 4096 else c // 64 if nm in ("nk", "nt") else c // 2 if wide == 16 else c % 256 // 32 if wide >= 256 else c
            nm = "%s%d" % (nm, c)
        key = now[0] + nm
        while key in now[1]:
            key += "+"
        now[1].add(key)
        ops.append(dict(eng=eng, kind=kind, args=args, w=w, r=r, n=n, key=key, rnd=now[2], **kw))

    def vcost(out, ins, tt=False):
        n = width(out)
        if out["off"] is not None:
            return ("S", n)
        if ins and ins[0]["off"] is not None:
            return ("Gt" if tt else "G", n)
        allb = two(out) and all(two(v) for v in ins)
        if tt and not any(isps(v) for v in ins):
            return ("tt2", n) if allb else ("c", 2 * n)
        return ("c", n / 2 if allb else n)

    def cp(out, a):
        add("v", "cp", (out, a), [out], [a], vcost(out, [a]))

    def tt(out, a, b, op, nm=None):
        add("v", "tt", (out, a, b, op), [out], [a, b], vcost(out, [a, b], True), nm)

    def ts(out, a, s1, op0, s2=None, op1=None, nm=None):
        add("v", "ts", (out, a, s1, s2, op0, op1), [out], [a, s1, s2], vcost(out, [a]), nm)

    def scan(out, d0, d1):
        add("v", "scan", (out, d0, d1), [out], [d0, d1], vcost(out, [d0, d1]))

    def ms(out, c):
        add("v", "ms", (out, c), [out], [], vcost(out, []))

    def tr(out, a):
        add("v", "tr", (out, a), [out], [a], vcost(out, [a]))

    def act(out, a, f, bias=0.0, scale=1.0, acc=None, extra=0.0, nm=None):
        add("a", "act", (out, a, f, bias, scale, acc), [out] + ([acc] if acc else []), [a, bias, scale],
            ("G" if a["off"] is not None else "c", width(out)), nm, extra=extra)

    def af(out, a, scale, bias=0.0):
        act(out, a, F.Identity, bias, scale)

    def mm(nm, lst, start=True, stop=True):
        n = sum(max(64, width(m[0])) * (1 if two(m[2]) else 4) for m in lst)
        add("p", "mm", lst, [m[0] for m in lst], [m[1] for m in lst] + [m[2] for m in lst], ("pe", n), nm, cnt=len(lst), start=start, stop=stop)

    def iota(out, pat, cm, base=0):
        add("g", "iota", (out, pat, cm, base), [out], [], ("c", 160 + 2 * width(out)))

    def asel(out, pat, cm):
        add("g", "asel", (out, pat, cm), [out], [out], ("c", 200 + 2 * width(out)))

    nd = [0, 0]

    def load(q, out, name, c0, c1, ns):
        add(q, "load", (out, name, c0, c1), [out], [], ("dma", ns), sem="d%d" % nd[0])
        nd[0] += 1

    def store(q, name, c0, c1, a, ns):
        add(q, "store", (name, c0, c1, a), [], [a], ("dma", ns), "%s%d" % (name, c0 // 512), sem="d%d" % nd[0], last=True)
        nd[0] += 1

    def send(dst, src, t):
        add("g", "send", (dst, src, t), [dst], [src], ("rem", 0), sem="r%d" % nd[1], cum=1)
        nd[1] += 1

    def col(j):
        return V("col", j, j + 1)

    OKP, N2, NKP, UC, PP, NH, VL, EE, DD, CN, AM, PK, MS = [(2, 256), (2, 256), (2, 384), (2, 384), (4, 0), (4, 128), (4, 128), (4, 256),
                                                            (4, 384), (6, 0), (6, 128), (6, 256), (6, 384)]

    def P(s, lo, hi):
        return V("ps%d" % (s[0] + lo // 128), s[1] + lo % 128, s[1] + lo % 128 + hi - lo)

    def sel(m, k):
        return V(m, 15 - k, 143 - k)

    load("a", V("pci", 0, 256), "pn", 0, 256, 2200)
    load("s", V("pci", 256, 512), "cn", 0, 256, 2200)
    load("s", V("X"), "lit", 0, 4096, 5500)
    load("a", V("ti", p1=8), "th", 0, 1, 2500)
    load("s", V("wi"), "wt", 0, 1, 5500)
    load("s", V("NN", 0, 256), "neg", 0, 256, 5500)
    iota(V("pi", 0, 1), [[0, 1]], 1)
    iota(V("Ja"), [[1, 16], [0, 2]], 0)
    iota(V("Mi"), [[1, 144]], 0)
    iota(V("Mg"), [[16, 8], [0, 16]], 0)
    iota(V("Ml"), [[0, 8], [1, 16]], 0)
    Jh, Mi = V("Ja", 0, 32, 2), V("Mi", 0, 128)
    ts(V("pi", 1, 2), V("pi", 0, 1), 15, A.bitwise_and)
    ts(V("pi", 2, 3), V("pi", 0, 1), 31, A.bitwise_and)
    cp(V("col", 0, 3), V("pi", 0, 3))
    ts(col(3), col(1), 16.0, A.mult)
    ts(V("oA"), V("Ja"), col(3), A.add)
    ts(V("oB"), Jh, 32.0, A.mult, col(2), A.add)
    for j, (nm, bias) in enumerate((("pp", 0.0), ("CF", 32.0))):
        a, b = V("t1", 512 * j, 512 * j + 512), V("t2", 512 * j, 512 * j + 512)
        cp(a, IND(V("pci", 256 * j, 256 * j + 256), V("oA")))
        tr(b, a)
        act(V(nm, 0, 256), IND(b, V("oB")), F.Identity, bias)
    act(V("nz", 0, 1), col(1), F.Sigmoid, -128.0, 256.0, extra=1300.0)
    iota(V("Ex"), [[1, 32], [0, 16]], 0)
    ts(V("Ex"), V("Ex"), col(2), A.is_equal, -1.0, A.mult)
    iota(V("BS"), [[0, 1152]], 0, 512)
    asel(V("BS"), [[-1, 9], [-16, 8], [0, 16]], 1)
    ts(col(15), col(0), col(1), A.subtract)
    af(col(4), col(15), 1.0, 15.0)
    af(col(5), col(0), 1.0, 1.0)
    ts(col(6), col(1), 15.0, A.not_equal)
    ts(col(7), col(1), 0.0, A.is_equal)
    af(col(8), col(7), 2304.0, -2176.0)
    ts(col(9), col(1), 1.0, A.is_equal, 8191.0, A.mult)
    af(col(10), col(9), 1.0, V("nz", 0, 1))
    ts(col(11), V("wi"), 0.0625, A.mult)
    af(col(12), col(1), 1.0, 15.0 / 32)
    af(col(13), col(1), 31.0, col(2))
    af(col(14), col(0), 16.0)
    af(col(16), col(7), 8191.0, 1.0)
    ts(col(17), col(1), 8.0, A.is_lt)
    af(col(18), col(7), 32.0)
    af(col(19), col(0), 1.0, 15.0)
    af(col(23), col(7), 2.0, -1.0)
    af(col(20), col(7), 1.0, -1.0)
    ts(V("oC"), V("Ja"), 16.0, A.mult, col(1), A.add)
    ts(V("oD"), Jh, col(13), A.add)
    af(V("bi"), Jh, 16.0, col(12))
    rs = 16 * max(cfg["QC"] if cfg["Q2"] else BC)
    ms(V("Rs", 0, rs), -256.0)
    ms(V("Rs", 0, rs, 16), 255.0)
    ms(V("on"), 1.0)
    pad = []
    for b, (lo, hi) in enumerate(chunks(BC)):
        ms(V("Dw", 16 * (lo + b), 16 * (lo + b) + 16), 255.0)
        ms(V("lp", 16 * (hi + b), 16 * (hi + b) + 16), 255.0)
        pad += [16 * b] * (hi - lo)
    ts(V("SZ"), V("Mi"), col(4), A.is_equal)
    if len(cfg["ST"]) < 4:
        af(V("SN"), V("SZ"), -1.0)
        af(V("SD"), V("SZ"), 2.0)
    ts(V("Gm"), V("Mg"), col(15), A.is_equal)
    for j, s, w in ((0, "1", col(16)), (1, "2", col(10)), (1, "E", col(7)), (2, "W", col(11))):
        if j in cfg["PS"]:
            af(V("K" + s), V("Gm"), w)
        else:
            af(V("S" + s), V("SZ"), w)
    if cfg["PS"]:
        ts(V("Cz"), V("Ml"), col(1), A.not_equal, -32768.0, A.mult)
        af(V("Dg"), Mi, 16.0)
        tt(V("Cb"), V("Dg"), V("Cz"), A.add)
        act(V("R0"), V("Ml"), F.Sigmoid, -128.0, 256.0)
    if len(cfg["PS"]) < 3:
        af(V("b16"), Jh, 256.0, col(3))
    ts(V("Zp"), V("Mi"), col(19), A.is_equal, col(17), A.mult)
    ts(V("Ib"), Mi, col(0), A.is_equal)
    af(V("In"), V("Ib"), -1.0)
    af(V("Ih"), V("Ib"), 0.5)
    ts(V("En"), V("Mg"), col(0), A.is_equal, -1.0, A.mult)
    af(V("Ep"), V("En"), -256.0)
    af(V("Em"), V("En"), 256.0)
    tt(V("Am"), V("Ib"), V("En"), A.add)
    af(V("If"), V("Ib"), 1.0)
    if not cfg["UA"]:
        ts(col(21), col(0), 1.0, A.is_equal, -37888.0, A.mult)
        ts(col(22), col(0), 0.0, A.is_equal, -83.0 * 2 ** 17, A.mult)
        af(col(22), col(22), 1.0, col(21))
        af(V("Uf"), V("Ib"), 2048.0)
        af(V("Ku"), V("on"), col(22))
    ts(V("Dt"), Mi, col(5), A.is_equal, col(6), A.mult)
    af(V("Dm"), V("Ib"), col(23))
    tt(V("Dm"), V("Dm"), V("Dt"), A.add)
    tt(V("Wm"), V("Ib"), sel("SZ", 0), A.subtract)
    af(V("DW"), V("Ib"), col(20))
    tt(V("DW"), V("DW"), V("Dt"), A.add)
    tt(V("nh", 0, 128), sel("SZ", 0), sel("SZ", 1), A.add)
    tt(V("DW"), V("DW"), V("nh", 0, 128), A.subtract)
    ts(V("Lm"), V("Ml"), col(1), A.is_ge, col(23), A.mult)
    tt(V("Lm"), V("Lm"), V("Gm"), A.mult)
    if cfg["PE"]:
        af(V("Ln"), V("Lm"), -1.0)
        af(V("Nf"), V("Ib"), -1.0)
        af(V("Kp"), V("Ib"), -896.0)
    af(V("Sa"), Mi, 0.0, col(7))
    ts(V("G8", p1=8), V("Mg", p1=8), V("col", 14, 15, p1=8), A.is_equal)
    cp(V("tf", 0, 1, p1=8), V("ti", p1=8))
    mm("TH", [(V("ps7", 320, 321), V("G8", p1=8), V("tf", 0, 1, p1=8))])
    plain, turned = len(cfg["ST"]) < 4, len(cfg["ST"]) > 0

    def c2(j):
        return V("cl2", j, j + 1)

    if plain:
        ts(V("tf", 2, 3), V("ps7", 320, 321), 65.0, A.add, col(17), A.mult)
        af(V("tf", 1, 2), V("tf", 2, 3), 1.0, -64.5)
        af(V("bz", 0, 1), V("tf", 1, 2), -256.0)
    if turned:
        cp(V("ai", 2, 3), V("ps7", 320, 321))
        ts(V("ai", 3, 4), V("ai", 2, 3), 63, A.bitwise_and)
        ts(c2(0), col(1), 1.0, A.is_equal, -1.0, A.mult)
        ts(c2(1), col(1), 2.0, A.is_equal)
        tt(c2(2), V("ai", 3, 4), V("ai", 2, 3), A.subtract)
        af(c2(3), c2(2), col(7), c2(1))
        ts(c2(4), V("ai", 3, 4), 0.5, A.add, c2(0), A.mult)
        af(c2(5), c2(4), 1.0, c2(3))
        ts(V("Tm"), V("Ml"), 8.0, A.is_ge, c2(1), A.is_equal)
        tt(V("Tm"), V("Tm"), V("Gm"), A.mult)
        af(V("Th"), V("Tm"), c2(5))
        af(V("GN"), V("Gm", 0, 128, 16), -1.0)
        af(V("GD"), V("Gm", 0, 128, 16), 2.0)
    af(V("Zn", 0, 128), V("BS", 1024, 1152), 1.0 / 1024)
    for h in range(2):
        tt(V("Zo", 128 * h, 128 * h + 128), V("Zn", 0, 128), sel("Zp", 8 * h), A.subtract)

    def turn_out(j, src, name, bias):
        a, b = V("t1", 512 * j, 512 * j + 512), V("t2", 512 * j, 512 * j + 512)
        act(a, IND(src, V("oC")), F.Identity, bias)
        tr(b, a)
        y = V("yo", 256 * j, 256 * j + 256)
        cp(y, IND(b, V("oD")))
        store("s", name, 0, 256, y, 2300)

    for lo, hi in chunks(BC):
        cp(V("pu", lo, hi), V("pp", lo, hi))
        act(P(PP, lo, hi), V("pp", lo, hi), F.Identity, -864.0)
    Xw = V("X")
    for t in range(RO):
        c0 = 256 * t
        now[:] = ["", set(), t]
        for lo, hi in chunks(HC):
            cf, u = V("CF", c0 + lo, c0 + hi), "%d" % (lo // 32)
            ts(V("cu", lo, hi), cf, -32.0, A.add)
            tt(V("tq", lo, hi), P(PP, lo, hi), cf, A.mult)
            if cfg["UA"]:
                act(P(UC, lo, hi), cf, F.Identity, -37888.0 - 83.0 * 2 ** 17, 2048.0, nm="UC" + u)
            else:
                mm("UC" + u, [(P(UC, lo, hi), V("Ku"), V("on", 0, hi - lo)), (P(UC, lo, hi), V("Uf"), cf)])
            tt(V("vi", lo, hi), P(UC, lo, hi), V("tq", lo, hi), A.add)
            ts(V("hi", lo, hi), V("vi", lo, hi), 5, A.arith_shift_right, 4095, A.bitwise_and)
            cp(V("hu", lo, hi), V("hi", lo, hi))
        for lo in (0, 128):
            mm("NT%d" % (lo // 32), [(P(MS, lo, lo + 128), V("NN", c0 + lo, c0 + lo + 128), V("Ib"))])
            act(V("nT", lo, lo + 128), P(MS, lo, lo + 128), F.Copy)
        for j, (lo, hi) in enumerate(chunks(FC)):
            r0, r1 = 16 * lo, 16 * hi
            for nm, ix, onv in (("xb", "pu", cfg["XV"]), ("yb", "cu", cfg["YV"])):
                if j in onv:
                    cp(V(nm, r0, r1), IND(Xw, V(ix, lo, hi)))
                else:
                    act(V(nm, r0, r1), IND(Xw, V(ix, lo, hi)), F.Copy)
            if j in cfg["FO"]:
                add("g", "fold", (V("mx", r0, r1), V("yb", r0, r1), V("xb", r0, r1), A.max), [V("mx", r0, r1)],
                    [V("yb", r0, r1), V("xb", r0, r1)], ("fold", r1 - r0), sem="f%d" % j, cum=t + 1)
            else:
                tt(V("mx", r0, r1), V("yb", r0, r1), V("xb", r0, r1), A.max)
            z = IND(Xw, V("hu", lo, hi))
            if j in cfg["ZA"]:
                act(V("zb", r0, r1), z, F.Copy)
                z = V("zb", r0, r1)
            elif j in cfg["ZV"]:
                cp(V("zb", r0, r1), z)
                z = V("zb", r0, r1)
            tt(V("lp", pad[lo] + r0, pad[lo] + r1), z, V("mx", r0, r1), A.min)
            if lo // 64 in cfg["ST"]:
                if hi % 64:
                    continue
                lo, r0 = hi - 64, r1 - 1024
            c = 128 * (lo // 128) + 2 * (lo % 64)
            sg = V("ps%d" % (2 + lo // 64 % 2), c, c + 2 * (hi - lo))
            if lo // 64 in cfg["ST"]:
                for u, (s, b) in enumerate((("GN", "xb"), ("GN", "yb"), ("GD", "mx"))):
                    mm("S%s%d" % (b[0], lo // 32), [(sg, V("on"), V("Th"))] * (u == 0)
                       + [(V(sg["name"], c + k, c + 128, 16), V(b, r0 + k, r1, 8), V(s)) for k in range(8)], u == 0, u == 2)
                act(V("nt", 2 * lo, 2 * hi), sg, F.Sigmoid, 0.0, 256.0)
                mm("St%d" % (lo // 32), [(sg, V("nt", 2 * lo, 2 * hi), V("Ib"))])
                act(V("nk", 2 * lo, 2 * hi), sg, F.Copy)
            else:
                for u, (s, b) in enumerate((("SN", "xb"), ("SN", "yb"), ("SD", "mx"))):
                    mm("S%s%d" % (b[0], lo // 32), [(sg, sel(s, k), V(b, r0 + k, r1, 8)) for k in range(8)], u == 0, u == 2)
                act(V("nk", 2 * lo, 2 * hi), sg, F.Sigmoid, V("bz", 0, 1), 256.0)
            for e in range(lo, hi, 32):
                bk, h, u = "ps%d" % (e // 32 % 2), 128 * (e // 128), "%d" % (e // 32)
                mm("Dn" + u, [(V(bk), V("nT", h, h + 128, p0=e - h, p1=e - h + 32), V("Ex", p0=e - h, p1=e - h + 32))], True, False)
                mm("Dk" + u, [(V(bk, s, 512, 8), V("BS", 128 * s, 128 * s + 128), V("nk", 2 * e, 2 * e + 64)) for s in range(8)], False, False)
                mm("Dl" + u, [(V(bk), V("Ib"), V("lp", pad[e] + 16 * e, pad[e] + 16 * e + 512))], False, True)
                scan(V("Dw", pad[e] + 16 + 16 * e, pad[e] + 16 + 16 * e + 512), V("Rs", 0, 512), V(bk))
            fw = min(cfg["FW"], hi - lo)
            for a in range(lo, hi, fw):
                d, f = V("Dw", pad[a] + 16 + 16 * a, pad[a] + 16 + 16 * (a + fw)), V("Bb", 1 + 16 * a, 1 + 16 * (a + fw))
                if a // 32 in cfg["FV"]:
                    ts(f, d, 0.0, A.is_ge)
                else:
                    act(f, d, F.Sigmoid, 128.0, 256.0)
            for a, b in chunks(cfg["QC"]):
                if lo < b <= hi:
                    mm("C1%d" % (a // 32), [(P(CN, a, b), sel("SZ", (k + 1) % 16), V("Bb", 1 + 16 * a + k, 1 + 16 * b, 16)) for k in range(16)])
        for b, (lo, hi) in enumerate(chunks(BC)):
            r0, r1, h0, h1, w, u = 16 * lo, 16 * hi, lo // 16, hi // 16, hi - lo, "%d" % (lo // 32)
            n_, cf, on = V("NN", c0 + lo, c0 + hi), V("CF", c0 + lo, c0 + hi), V("on", 0, w)

            def L(name):
                return V(name, lo, hi)

            def picks(j, srcs, base):
                if j not in cfg["PS"]:
                    o = P(PK, lo, lo + h1 - h0)
                    mm("K%d%s" % (j, u), ([(o, V("Ib"), V("b16", 0, h1 - h0))] if base else [])
                       + [(o, sel("S" + s, il), V(x["name"], x["c0"] + il, x["c1"], 16)) for s, x in srcs for il in range(16)])
                    return o
                mm("K%d%s" % (j, u), [(P(PK, lo, hi), V("Ib"), V("Cb" if base else "Cz", 0, w))] + [(P(PK, lo, hi), V("K" + s), x) for s, x in srcs])
                add("v", "scan2", (L("pk"), V("R0", 0, w), P(PK, lo, hi)), [L("pk")], [V("R0", 0, w), P(PK, lo, hi)], ("c", w), "k%d%s" % (j, u))
                return V("pk", lo + 15, hi, 16)

            nk = [V("nk", 2 * lo + h, 2 * hi, 2) for h in range(2)]
            mm("OK" + u, [(P(OKP, lo, hi), V("Zo", 128 * h, 128 * h + 128), nk[h]) for h in range(2)])
            mm("NK" + u, [(P(NKP, lo, hi), sel("Zp", 8 * h), nk[h]) for h in range(2)])
            tt(L("w1"), P(OKP, lo, hi), L("hi"), A.mult)
            tt(L("w2"), P(NKP, lo, hi), L("pp"), A.mult)
            mm("DA" + u, [(P(DD, lo, hi), V("Dm"), L("w1")), (P(DD, lo, hi), V("Dm"), L("w2"))])
            act(L("D1"), P(DD, lo, hi), F.Identity, col(18))
            act(L("nb"), P(CN, lo, hi), F.Sigmoid, -2176.0, 256.0, acc=V("acc", b, b + 1) if t < RO - 1 else None)
            o = picks(0, [("1", L("nb"))], True)
            ts(V("i1", h0, h1), o, 16.0 * w, A.min)
            law = IND(V("lp", r0 + 16 * b, r1 + 16 * b + 16), V("i1", h0, h1))
            seed = V("Bb", r0, r1, 16)
            if b in cfg["SA"]:
                act(L("lk"), law, F.Copy)
                mm("DK" + u, [(P(MS, lo, hi), V("In"), n_), (P(MS, lo, hi), V("Ib"), L("lk"))])
                act(seed, P(MS, lo, hi), F.Sigmoid, 128.0, 256.0, nm="sd" + u)
            elif b in cfg["SM"]:
                tt(seed, law, n_, A.is_ge, nm="sd" + u)
                act(L("lk"), law, F.Copy)
                mm("DK" + u, [(P(MS, lo, hi), V("In"), n_), (P(MS, lo, hi), V("Ib"), L("lk"))])
                act(L("dk"), P(MS, lo, hi), F.Copy)
            else:
                tt(L("dk"), law, n_, A.subtract)
                ts(seed, L("dk"), 0.0, A.is_ge, nm="sd" + u)
            for a, e in chunks(cfg["QC"]) if cfg.get("Q2") else [(lo, hi)]:
                if lo <= a < hi:
                    scan(V("B2", 16 * a, 16 * e), V("Rs", 0, 16 * (e - a)), V("Bb", 16 * a, 16 * e))
                    mm("C2%d" % (a // 32), [(P(CN, a, e), sel("SZ", j + 1), V("B2", 16 * a + j, 16 * e, 16)) for j in range(15)])
            mm("A1" + u, [(P(AM, lo, hi), V("Am"), L("nb"))])
            tt(L("ta"), P(AM, lo, hi), L("D1"), A.mult)
            mm("DB" + u, [(P(DD, lo, hi), V("If"), L("D1")), (P(DD, lo, hi), V("DW"), L("ta"))])
            act(L("D2"), P(DD, lo, hi), F.Copy)
            if b not in cfg["MA"]:
                mm("NH" + u, [(P(NH, lo, hi), V("Ib"), n_), (P(NH, lo, hi), V("Ep"), L("nb"))])
                act(L("nh"), P(NH, lo, hi), F.Identity, -256.0)
            if cfg["PE"]:
                mm("EE" + u, [(P(EE, lo, hi), V("If"), cf), (P(EE, lo, hi), V("Ln"), L("D2"))])
            mm("Na" + u, [(P(N2, lo, hi), V("Lm"), L("D2"))], True, False)
            if cfg["PE"]:
                mm("Pa" + u, [(P(PP, lo, hi), V("Kp"), on), (P(PP, lo, hi), V("If"), cf)], True, False)
            act(L("kp"), P(CN, lo, hi), F.Sigmoid, col(8), 256.0)
            mm("A2" + u, [(P(AM, lo, hi), V("En"), L("nb")), (P(AM, lo, hi), V("Ib"), L("kp"))])
            tt(L("tb"), P(AM, lo, hi), L("D2"), A.mult)
            mm("Nb" + u, [(P(N2, lo, hi), V("Wm"), L("tb"))], False, True)
            sc = V("SC", c0 + lo, c0 + hi)
            act(sc, P(N2, lo, hi), F.Copy)
            send(V("CF", c0 + 256 + lo, c0 + 256 + hi), sc, t)
            if cfg["PE"]:
                tt(L("tc"), P(EE, lo, hi), L("kp"), A.mult)
                mm("Pb" + u, [(P(PP, lo, hi), V("Nf"), L("tc"))], False, False)
                mm("Pc" + u, [(P(PP, lo, hi), V("Wm"), L("tb"))], False, True)
                if t < RO - 1:
                    ts(L("pu"), P(PP, lo, hi), 864.0, A.add)
                act(L("pp"), P(PP, lo, hi), F.Identity, 864.0)
            else:
                tt(P(EE, lo, hi), P(N2, lo, hi), cf, A.subtract, nm="u1" + u)
                tt(P(EE, lo, hi), P(EE, lo, hi), L("kp"), A.mult, nm="u2" + u)
                tt(L("tc"), P(EE, lo, hi), cf, A.add)
                if t < RO - 1:
                    ts(L("pu"), L("tc"), -32.0, A.add)
                    act(P(PP, lo, hi), L("tc"), F.Identity, -896.0, nm="PP" + u)
                act(L("pp"), L("tc"), F.Identity, -32.0)
            o = picks(1, [("E", L("nb")), ("2", L("kp"))], True)
            ts(V("i2", h0, h1), o, 16.0 - 8192.0, A.add, 0.0, A.max)
            dw = IND(V("Dw", r0 + 16 * b, r1 + 16 * b + 16), V("i2", h0, h1))
            if b in cfg["SA"]:
                act(L("dp"), dw, F.Copy)
                tt(L("DM"), P(MS, lo, hi), L("dp"), A.min)
            else:
                tt(L("DM"), dw, L("dk"), A.min)
            o = picks(2, [("W", n_), ("W", L("DM"))], False)
            tt(V("qq", h0, h1), o, V("bi", 0, h1 - h0), A.subtract)
            tt(V("ff", h0, h1), o, V("qq", h0, h1), A.subtract)
            ts(V("i3", h0, h1), V("ff", h0, h1), 16.0, A.mult)
            mm("VL" + u, [(P(VL, lo, hi), V("Ib"), n_), (P(VL, lo, hi), V("Ih"), L("DM"))])
            if b in cfg["VA"]:
                af(L("vf"), P(VL, lo, hi), 1.0 - 2.0 ** -10, 12582912.0)
                af(L("vb"), L("vf"), 1.0, -12582912.0)
                cp(IND(V("X", r0, r1), V("i3", h0, h1)), L("vb"))
            else:
                ts(L("vl"), P(VL, lo, hi), -0.25, A.add)
                cp(IND(V("X", r0, r1), V("i3", h0, h1)), L("vl"))
            sm = V("SM", c0 + lo, c0 + hi)
            if b in cfg["MA"]:
                for nm, sg in (("r1", "Ib"), ("r2", "In")):
                    mm(nm.upper() + u, [(P(AM, lo, hi), V("Em"), L("nb")), (P(AM, lo, hi), V(sg), L("DM"))])
                    act(L(nm), P(AM, lo, hi), F.Relu)
                mm("PA" + u, [(P(MS, lo, hi), V("Ib"), n_), (P(MS, lo, hi), V("Ib"), L("r1")), (P(MS, lo, hi), V("In"), L("r2"))])
                act(sm, P(MS, lo, hi), F.Copy)
            else:
                mm("PA" + u, [(P(MS, lo, hi), V("Em"), L("nb")), (P(MS, lo, hi), V("Ib"), n_), (P(MS, lo, hi), V("Ib"), L("DM"))])
                tt(sm, P(MS, lo, hi), L("nh"), A.max)
            send(V("NN", c0 + 256 + lo, c0 + 256 + hi), sm, t)
            if t == RO - 1:
                store("s", "yx", r0, r1, V("X", r0, r1), 1800 + 4200 * (hi - lo) // NL)
        if t < RO - 1:
            o = V("ps7", 128, 129)
            mm("AS", [(o, V("Sa"), V("acc", b, b + 1)) for b in range(len(BC))])
            cp(V("ai", 0, 1), o)
            ts(V("ai", 1, 2), V("ai", 0, 1), 63, A.bitwise_and)
            if plain:
                ts(V("bz", 0, 1), V("ai", 1, 2), V("tf", 1, 2), A.add, -256.0, A.mult)
            if turned:
                ts(V("bz", 1, 2), V("ai", 1, 2), c2(0), A.mult, c2(5), A.add)
                af(V("Th"), V("Tm"), V("bz", 1, 2))
    now[:] = ["e", set(), RO]
    turn_out(0, V("pp"), "yp", 0.0)
    turn_out(1, V("CF", 256 * RO, 256 * RO + 256), "yc", -32.0)
    store("a", "yn", 0, 256, V("NN", 256 * RO, 256 * RO + 256), 2200)

    seen, starts, closed = {}, {}, {}
    for i, o in enumerate(ops):
        dep = set()
        for kind, lst in (("r", o["r"]), ("w", o["w"])):
            for nm, a, b in lst:
                for (j, k2, c, d) in seen.get(nm, ()):
                    if c < b and a < d and (kind == "w" or k2 == "w"):
                        dep.add(j)
        for nm, a, b in o["w"]:
            seen[nm] = [e for e in seen.get(nm, ()) if not (a <= e[2] and e[3] <= b)] + [(i, "w", a, b)]
        for nm, a, b in o["r"]:
            seen.setdefault(nm, []).append((i, "r", a, b))
        if o["kind"] == "mm":
            bk = o["w"][0][0]
            if o["start"]:
                dep.update(closed.get(bk, ()))
                if not o["stop"]:
                    dep.update(starts.pop(bk, ()))
                else:
                    starts.setdefault(bk, []).append(i)
            elif o["stop"]:
                closed[bk] = [i]
        dep.discard(i)
        o["dep"] = dep
        o["banks"] = sorted(set(nm for nm, a, b in o["r"] + o["w"] if nm.startswith("ps")))
    return ops


def times(o, C):
    k, n = o["n"]
    if k == "dma":
        return 100.0, float(n)
    if k == "rem":
        return 400.0, C["rem"]
    if k == "fold":
        return 400.0, 2 * C["rem"] + n * C["fb"]
    if k == "pe":
        d = n * C["pe"] + C["fp"] * o["cnt"]
        return d, d + 60.0
    f = C["fa"] if o["eng"] == "a" else C["fv"]
    per = {"G": C["G"], "Gt": C["G"] + C["Gop"], "S": C["S"], "tt2": C["tt2"], "c": 1.0}[k]
    d = f + max(n * per, C["mn"]) * C["cyc"] + o.get("extra", 0.0)
    return d, d


def in_order(ops):
    names = ORDER.split()
    place = {x.strip("<>"): j + len(names) * (x.count("<") - x.count(">")) for j, x in enumerate(names)}
    rank = [len(names) * min(max(o["rnd"], 0), RO - 1) + place.get(o["key"], 0) for o in ops]
    left = [len(o["dep"]) for o in ops]
    succ = [[] for _ in ops]
    for i, o in enumerate(ops):
        for j in o["dep"]:
            succ[j].append(i)
    at, first = -2.0 * len(names), {}
    for x in SETUP.split():
        if x[0] == "@":
            at = place[x[1:]] - 0.5
        else:
            at += 0.001
            first["s" + x] = at
    for i, o in enumerate(ops):
        if o["rnd"] < 0:
            rank[i] = first.get(o["key"], -3.0 * len(names))
    ready, out = [i for i in range(len(ops)) if not left[i]], []
    while ready:
        i = min(ready, key=lambda j: (rank[j], j))
        ready.remove(i)
        out.append(i)
        for j in succ[i]:
            left[j] -= 1
            if not left[j]:
                ready.append(j)
    return out


def waits(ops, order):
    csem = {"v": "cv", "a": "ca", "p": "cp", "g": "cg"}
    cnt, known, mark, clock, lastb, out = {}, {}, {}, {}, {}, {}
    for i in order:
        o = ops[i]
        dep = set(o["dep"])
        for b in o["banks"]:
            for e, j in lastb.get(b, {}).items():
                if e != o["eng"]:
                    dep.add(j)
        kn = known.setdefault(o["eng"], {})
        ws = []
        for j in sorted(dep, key=lambda j: -mark[j][2]):
            s, c = mark[j][0], mark[j][1]
            if kn.get(s, 0) >= c:
                continue
            ws.append((s, c))
            kn[s] = c
            for s2, c2 in clock[j].items():
                if kn.get(s2, 0) < c2:
                    kn[s2] = c2
        out[i] = ws
        if "sem" in o:
            mark[i] = (o["sem"], o.get("cum", 16), len(mark))
        else:
            s = csem[o["eng"]]
            cnt[s] = cnt.get(s, 0) + 1
            mark[i] = (s, cnt[s], len(mark))
        clock[i] = {} if "cum" in o else dict(kn)
        for b in o["banks"]:
            lastb.setdefault(b, {})[o["eng"]] = i
    return out, mark, cnt


PLAN = {}


def plan():
    if not PLAN:
        ops = build(CFG)
        order = in_order(ops)
        PLAN["p"] = (ops, order) + waits(ops, order)
    return PLAN["p"]


def helpers(T, topo):
    out = {}
    for c in T.cores:
        free = [x for x in topo.cores_of(c) if T.rank_of(x) is None and x not in out.values()]
        out[c] = min(free, key=lambda x: (topo.die(x) != topo.die(c), x))
    return out


def emit(o, ws, mark, g, core, T, topo):
    q = {"v": g.vector, "a": g.scalar, "p": g.tensor, "g": g, "s": g.sync}[o["eng"]]
    rank = T.rank_of(core)
    n = len(T.cores)
    lanes = len(topo.engines(T.cores[rank - 1], core))
    for s, c in ws:
        q.wait_ge(T.sem[s], c * lanes if s[0] in "rf" else c)
    k, a = o["kind"], [ap(T, x) for x in o["args"]]
    if k == "cp":
        ins = q.tensor_copy(a[0], a[1])
    elif k == "tt":
        ins = q.tensor_tensor(a[0], a[1], a[2], a[3])
    elif k == "ts":
        ins = q.tensor_scalar(a[0], a[1], a[2], None, a[4]) if a[5] is None else q.tensor_scalar(a[0], a[1], a[2], a[3], a[4], a[5])
    elif k == "scan":
        ins = q.tensor_tensor_scan(a[0], a[1], a[2], 0.0, A.max, A.min)
    elif k == "scan2":
        ins = q.tensor_tensor_scan(a[0], a[1], a[2], 0.0, A.mult, A.max)
    elif k == "ms":
        ins = q.memset(a[0], a[1])
    elif k == "tr":
        ins = q.transpose(a[0], a[1])
    elif k == "act":
        if a[2] in (F.Copy, F.Relu):
            ins = q.activation(a[0], a[1], a[2])
        elif a[5] is None:
            ins = q.activation(a[0], a[1], a[2], bias=a[3], scale=a[4])
        else:
            ins = q.activation(a[0], a[1], a[2], bias=a[3], scale=a[4], accum_out=a[5])
    elif k == "mm":
        for j, m in enumerate(a):
            ins = q.matmul(ap(T, m[0]), ap(T, m[1]), ap(T, m[2]), j == 0 and o["start"], j == len(a) - 1 and o["stop"])
    elif k == "iota":
        if SCRATCH[o["args"][0]["name"]][2] == I32:
            ins = q.iota(a[0], a[1], a[3], a[2])
        else:
            ins = q.iota(a[0], a[1], a[3], a[2], allow_small_or_imprecise_dtypes=True)
    elif k == "asel":
        ins = q.affine_select(a[0], a[0], a[1], A.is_equal, 0.0, 0, a[2])
    elif k == "load":
        ins = q.dma_start(a[0], T[a[1]][:])
    elif k == "store":
        ins = q.dma_start(T[a[0]][:, a[1]:a[2]], a[3])
    elif k == "fold":
        dst = helpers(T, topo)[core]
        rid, pid, _ = topo.addr(dst)
        q.remote_dma_fused([RemoteDMATransfer(dst_ids=[DstId(rid=rid, pnc=pid)], dma_engine_mask=topo.mask(core, dst), remote_sem=T.sem[o["sem"]],
                                              srcs=[a[1], a[2]], dsts=[a[0]], alu_op=2)], local_sem=T.sem["loc"])
        return len(topo.engines(core, dst))
    else:
        dst = T.cores[(rank + 1 + a[2] % 3) % n]
        rid, pid, _ = topo.addr(dst)
        q.remote_dma(a[0], a[1], T.sem[o["sem"]], T.sem["loc"], pid, rid, topo.mask(core, dst))
        return len(topo.engines(core, dst))
    ins.then_inc(T.sem[mark[0]], 16 if "sem" in o else 1)
    return 0


def rank_program(g, core, T, topo):
    ops, order, ws, mark, cnt = plan()
    loc = 0
    if T.rank_of(core) is None:
        for c, h in helpers(T, topo).items():
            if h == core:
                rid, pid, _ = topo.addr(c)
                for i in order:
                    o = ops[i]
                    if o["kind"] == "fold":
                        g.wait_ge(T.sem[o["sem"]], o["cum"] * len(topo.engines(c, h)))
                        x = ap(T, o["args"][0])
                        g.remote_dma(x, x, T.sem[o["sem"]], T.sem["loc"], pid, rid, topo.mask(h, c))
                        loc += len(topo.engines(h, c))
        if loc:
            g.wait_ge(T.sem["loc"], loc)
        return
    for i in order:
        loc += emit(ops[i], ws[i], mark[i], g, core, T, topo)
    for s, c in cnt.items():
        g.wait_ge(T.sem[s], c)
    g.wait_ge(T.sem["loc"], loc)
    for o in ops:
        if o.get("last"):
            g.wait_ge(T.sem[o["sem"]], 16)
